import numpy as np, ml_dtypes
CORES = [2,3,42,43,82,83,122,123]
N = 8
import mx_ref
BF = ml_dtypes.bfloat16
def gentries(a):
    return np.ascontiguousarray(a.reshape(8, 16, -1).transpose(0, 2, 1)).reshape(8, -1)
def gtable(e):
    e = np.asarray(e); return np.ascontiguousarray(e.reshape(8, -1, 16).transpose(0, 2, 1)).reshape(128, -1).astype(np.int32)
def gcols(t, e):
    v = np.concatenate([t.reshape(8, 16, -1, 4), np.zeros((8, 16, 1, 4), BF)], axis=2)
    return np.ascontiguousarray(np.stack([v[g][:, e[g]] for g in range(8)])).reshape(128, -1)
def gpick(z, e):
    return np.concatenate([z[16 * g:16 * g + 16][:, e[g]] for g in range(8)])
def tile(rs):
    return np.stack(rs, axis=2).reshape(128, -1).astype(BF)
def pick(q, e):
    c = np.concatenate([q[0].reshape(128, -1, 4), np.zeros((128, 1, 4), np.uint8)], axis=1); s = np.concatenate([q[1], np.ones((16, 1), np.uint8)], axis=1)
    return (np.ascontiguousarray(c[:, e].reshape(128, -1)), np.ascontiguousarray(s[:, e]))
def join(*qs):
    return (np.concatenate([q[0] for q in qs], axis=1), np.concatenate([q[1] for q in qs], axis=1))
def put(q, e, v):
    c, s = q[0].reshape(128, -1, 4).copy(), q[1].copy(); c[:, e] = v[0].reshape(128, -1, 4); s[:, e] = v[1]
    return (c.reshape(128, -1), s)
def pk(c, s):
    return (np.ascontiguousarray(c), mx_ref.live(s))
def emit(q):
    return q[0], q[1]
def packed(v, rng):
    q = [mx_ref.quantize(np.ascontiguousarray(v[r])) for r in range(N)]
    return np.stack([a for a, b in q]), np.stack([mx_ref.plane(b, rng) for a, b in q])
def values_of_codes():
    e, c = np.zeros((128, 128, 4), np.float32), np.zeros((128, 2, 4), np.uint8)
    e[np.arange(128), np.arange(128), 0] = 1
    c[:127, :, 0] = np.arange(256).reshape(2, 128).T[:127]
    return mx_ref.matmul(mx_ref.quantize(e.reshape(128, 512).astype(BF)), (c.reshape(128, 8), np.full((16, 2), 127, np.uint8))).T.reshape(-1).astype(np.float64)
CODE_VALUE, SCALE_VALUE = values_of_codes(), 2.0 ** (np.arange(256) - 127.0)
def decode(q):
    return (CODE_VALUE[q[0]].reshape(16, 8, -1, 4) * SCALE_VALUE[q[1]][:, None, :, None] + 0.0).reshape(128, -1).astype(np.float32)
def f(rng, *shape):
    return mx_ref.flush((rng.standard_normal(shape, dtype=np.float32) * np.exp2(rng.integers(-2, 3, shape[:-1] + (1,)))).astype(BF))
def wide(rng, *shape, cols=0):
    v = rng.standard_normal(shape, dtype=np.float32) * np.exp2(rng.integers(-12, 13, shape)).astype(np.float32)
    if cols: v *= np.repeat(np.exp2(rng.integers(-cols, cols + 1, shape[:-2] + (1, shape[-1] // 4))) * (rng.random(shape[:-2] + (1, shape[-1] // 4)) > 0.0625), 4, axis=-1).astype(np.float32)
    return mx_ref.flush(v.astype(BF))
C = 384
STEP = [1, 2, 4]
def at(t, e):
    return np.take_along_axis(t, e, axis=1)
def ext(e):
    return np.concatenate([e, np.full((len(e), 1), C)], axis=1)
def numbers_of(rng):
    return {"x": np.array(f(rng, N, 128, 4 * C)), "u": np.array(f(rng, N, 128, 512)), "v": np.array(f(rng, N, 128, 512))}
def trees(rng, kind, o=None):
    n, kind = 8 * N, kind.reshape(-1)
    t = np.arange(n)
    if o is None: o = rng.permuted(np.tile(np.arange(C), (n, 1)), axis=1)
    free = np.tile(np.arange(C + 1), (n, 1))
    e = np.full((3, n, C), C)
    for i in range(1, C):
        k = rng.integers(0, i + 1, n)
        side = np.where(kind == 1, rng.integers(0, 2, n), kind - 3)
        slot = np.where(kind == 0, free[t, k], np.where(kind == 2, i - 1, 2 * i - 2 + side))
        free[t, k] = 2 * i
        free[:, i + 1] = 2 * i + 1
        a = o[t, slot // 2]
        e[0, t, o[:, i]] = a
        e[1 + slot % 2, t, a] = o[:, i]
    return e.reshape(3, N, 8, C)
def depths(p):
    h = ext(p.reshape(8 * N, C))
    d = (h < C).astype(np.int64)
    for k in range(9):
        d = d + at(d, h)
        h = at(h, h)
    return d[:, :C].reshape(N, 8, C)
def stored(e):
    return {k: np.stack([gtable(e[i, r]) for r in range(N)]) for i, k in enumerate(("up", "lf", "rt"))}
def lists(rng):
    return stored(trees(rng, np.zeros((N, 8), np.int64)))
def mixed(rng):
    return np.stack([rng.permutation([0, 0, 0, 1, 1, 2, 3, 4]) for r in range(N)])
def layers(rng, still=[]):
    w = np.array(f(rng, N, 128, 2048)).reshape(N, 8, 16, 4, 8, 16, 4)
    for i in still:
        w[:, :, i] = 0
        w[:, :, :, :, :, i] = 0
    return w
def weights(rng, w):
    c, p = packed(np.ascontiguousarray(w).reshape(N, 128, 2048), rng)
    return {"wc": c, "ws": p}
def setup_inputs(rng):
    return {**numbers_of(rng), **lists(rng), **weights(rng, layers(rng))}
def setup_inputs_ties(rng):
    d = numbers_of(rng)
    o = rng.permutation(N) % 4
    kind = mixed(rng)
    kind[o == 3] = 1
    e = trees(rng, kind)
    h = depths(e[0])
    k = rng.integers(0, 4, (N, 8, C))
    k[o == 0] = 5
    k[o == 1] = h[o == 1]
    k[o == 3] = h[o == 3] % 3 == 1
    x = d["x"].reshape(N, 8, 16, C, 4)
    x[:, :, :3] = 0
    u = d["u"].reshape(N, 128, 128, 4)
    u[:, :, ::16] = 0
    for i in range(3):
        x[:, :, i, :, 0] = (k // 8 ** i % 8).astype(np.float32).astype(BF)
        for c in range(0, 128, 16): u[:, c + i, c, 0] = 8.0 ** i
    return {"x": x.reshape(N, 128, 4 * C), "u": u.reshape(N, 128, 512), "v": d["v"], **stored(e), **weights(rng, layers(rng, [0, 1, 2]))}
def setup_inputs_near(rng):
    d = numbers_of(rng)
    x = d["x"].astype(np.float32).reshape(N, 8, 16, C, 4)
    x[:, :, 0] = 0
    x[:, :, 8:] = 0
    u = d["u"].reshape(N, 128, 128, 4)
    u[:, :, ::16] = 0
    o = (np.arange(N) + rng.integers(4)) % 4
    for r in range(N):
        c = np.where(rng.permutation(8)[:, None] < 4, rng.choice([-1.0, 1.0], (8, 1)), rng.choice([-1.0, 1.0], (8, C)))
        s = rng.integers(0, 16, (8, C))
        digits = ((s[:, :, None] >> np.arange(4)) & 1) * np.exp2(np.arange(4) - 23.0)
        if o[r] < 2:
            x[r, :, 0, :, 0] = c
            x[r, :, 8] = digits
            x[r, :, 11, :, 0] = c * 2.0 ** -10
        elif o[r] == 2: x[r, :, 8] = digits * rng.choice([-1.0, 1.0], (8, C, 1))
        else:
            a = rng.choice([-1.0, 1.0], (8, 1)) * 2.0 ** -30
            x[r, :, 8, :, 0] = np.where(s < 8, 1.25, 0.0) * a
            x[r, :, 9, :, 0] = np.where(s < 8, 0.0, 1.125) * a
            for g in rng.permutation(8)[:4]:
                e = rng.choice([-1.0, 1.0], C) * 2.0 ** -30
                x[r, g, 8, :, 0] = 1.25 * e
                x[r, g, 9, :, 0] = -1.125 * e
        if o[r] > 1: x[r, :, 12, :, 0] = rng.choice([1.0, 1.5], (8, C)) * 2.0 ** -30
        place = [0, C - 1, int(rng.integers(C)), int(rng.integers(C))]
        for g, j in zip(rng.permutation(8)[:4], place): x[r, g, 0, j, 0] = 2.0 ** 29 * rng.choice([-1.0, 1.0])
        k = 1.0 if o[r] == 0 else 2.0 ** -30
        for h in range(0, 128, 16):
            u[r, h, h, 0] = k if o[r] < 2 else 1.0
            if o[r] < 2: u[r, h + 11, h, 0] = k
            if o[r] < 3: u[r, h + 8, h] = k
            else:
                u[r, h + 8, h, 0] = k
                u[r, h + 9, h, 0] = 1.125 * k
                u[r, h + 10, h, 0] = k
    w = layers(rng, [0, 8, 9, 10, 11, 12, 13, 14, 15])
    for g in range(8): w[:, g, 12, 0, g, 10, 0] = 2.0 ** -8
    return {"x": x.reshape(N, 128, 4 * C).astype(BF), "u": u.reshape(N, 128, 512), "v": d["v"], **stored(trees(rng, mixed(rng))), **weights(rng, w)}
def setup_inputs_odd(rng):
    d = numbers_of(rng)
    o = rng.permutation(N) % 2
    x = (1.0 + (2 * rng.integers(0, 64, (N, 16, 8, C, 4)) + 1) * 2.0 ** -7) * np.exp2(-rng.integers(0, 7, (N, 16, 8, C, 4)).astype(np.float64)) * rng.choice([-1.0, 1.0], (N, 16, 8, C, 4))
    x[:, :, 0, :, 0] = rng.choice([1.96875, 1.875], (N, 16, C)) * 2.0 ** 8 * rng.choice([-1.0, 1.0], (N, 16, 1))
    u = d["u"].reshape(N, 16, 8, 128, 4)
    u[:, :, 0, ::16] = 0
    for r in range(N):
        if o[r]: continue
        for g, i in enumerate(rng.permutation(8) % 2):
            x[r, 2 * g, 1, :, 0] = (8 + rng.integers(0, 2, C)) * 2.0 ** (i - 8.0)
            u[r, :, :, 16 * g] = 0
            u[r, 2 * g, 1, 16 * g, 0] = 1.0
    return {"x": x.astype(np.float32).reshape(N, 128, 4 * C).astype(BF), "u": u.reshape(N, 128, 512), "v": d["v"], **lists(rng), **weights(rng, layers(rng, [0, 8]))}
def setup_inputs_ends(rng):
    d = numbers_of(rng)
    o = (np.arange(N) + rng.integers(4)) % 4
    big = (o < 2)[:, None, None, None]
    def sized(*n):
        return np.where(big, (0.955 + 0.02 * rng.random((N,) + n)) * 2.0 ** 30, (1.0 + 0.125 * rng.integers(0, 8, (N,) + n)) * 2.0 ** -30)
    s = rng.choice([-1.0, 1.0], (N, 128, C, 4))
    s[o == 1] = rng.choice([-1.0, 1.0], (N, 1, C, 1))[o == 1]
    s[o == 3] = rng.choice([-1.0, 1.0], (N, 128, 1, 4))[o == 3]
    s[o % 2 == 0] = -1
    x = s * sized(128, C, 4)
    h = np.stack([rng.permutation(8) for r in range(N)])
    u = d["u"].reshape(N, 128, 128, 4)
    u[:, :, ::16] = (np.where(h < 2, 0.0, h % 2 * 2.0 - 1.0)[:, None, :, None] * sized(128, 8, 4)).astype(np.float32).astype(BF)
    v = rng.choice([-1.0, 1.0], (N, 128, 128, 4)) * sized(128, 128, 4)
    w = np.zeros((N, 128, 4, 128, 4), np.float32)
    i = np.arange(128)
    for b in range(4): w[:, i, b, i, b] = np.array([-0.125, -0.125, -2.0 ** -8, 2.0 ** 4])[o][:, None]
    kind = np.stack([rng.permutation([0, 1, 2, 2, 3, 3, 4, 4]) for r in range(N)])
    fall = np.stack([rng.permutation(8) % 2 for r in range(N)]).reshape(-1, 1)
    k = np.tile(np.arange(C), (8 * N, 1))
    return {"x": x.astype(np.float32).reshape(N, 128, 4 * C).astype(BF), "u": u.reshape(N, 128, 512), "v": v.astype(np.float32).reshape(N, 128, 512).astype(BF), **stored(trees(rng, kind, np.where(fall == 0, k, C - 1 - k))), **weights(rng, w.astype(BF))}
def setup_inputs_spread(rng):
    d = setup_inputs(rng)
    d["x"] = wide(rng, N, 128, 4 * C, cols=6)
    return d
def check_inputs(d):
    b = []
    for k in ("x", "u", "v"):
        a = np.abs(d[k].astype(np.float32))
        if not (np.isfinite(a).all() and ((a == 0) | (a >= 2.0 ** -30) & (a <= 2.0 ** 30)).all()): b.append("a value of " + k)
    bad = [k for k in ("up", "lf", "rt") if not ((d[k] >= 0) & (d[k] <= C)).all()]
    b += ["an entry of " + k for k in bad]
    none, least, most = [emit(mx_ref.quantize(np.full((128, 16), k, np.float32).astype(BF)))[1][0, 0] for k in (0.0, 2.0 ** -8, 2.0 ** 8)]
    own = np.arange(C + 1)
    for r in range(N):
        if ((d["wc"][r] == 0x7F) | (d["wc"][r] == 0xFF)).any(): b.append("wc: a code that is no number")
        s = mx_ref.live(d["ws"][r])
        if ((s != none) & ((s < least) | (s > most))).any(): b.append("ws: a scale out of range")
        if bad: continue
        p, l, e = [ext(gentries(d[k][r])) for k in ("up", "lf", "rt")]
        ok = (np.sum(p[:, :C] == C, axis=1) == 1).all() and (np.sum(l < C, axis=1) + np.sum(e < C, axis=1) == C - 1).all()
        ok = ok and ((l == C) | (l != e)).all() and all(((k == C) | (at(p, k) == own)).all() for k in (l, e))
        for k in range(9): p = at(p, p)
        if not (ok and (p == C).all()): b.append("up, lf, rt: not a tree")
    return b
def rotated(s, p, l, r):
    own = np.tile(np.arange(C + 1), (8, 1))
    w = np.concatenate([s, np.zeros((8, 1), np.float32)], axis=1)
    gain = np.where(p < C, np.maximum(w - at(w, p), np.float32(0)), np.float32(0))
    def better(a, b):
        i, j = at(gain, a), at(gain, b)
        return np.where((i > j) | (i == j) & (a < b), a, b)
    child = better(l, r)
    best = better(better(own, child), better(at(child, l), at(child, r)))
    z = at(p, p)
    g, v = np.nonzero((gain > 0) & (best == own) & (at(best, p) == own) & ((z == C) | (at(best, z) == own)))
    y, z = p[g, v], z[g, v]
    left, high = l[g, y] == v, l[g, z] == y
    c = np.where(left, r[g, v], l[g, v])
    a, b, e = p.copy(), l.copy(), r.copy()
    a[g, c], a[g, y], a[g, v] = y, v, z
    b[g, y], e[g, y] = np.where(left, c, l[g, y]), np.where(left, r[g, y], c)
    b[g, v], e[g, v] = np.where(left, l[g, v], y), np.where(left, y, r[g, v])
    b[g, z], e[g, z] = np.where(high, v, l[g, z]), np.where(high, r[g, z], v)
    for k in (a, b, e): k[:, C] = C
    return a, b, e
def reference(x, u, v, up, lf, rt, wc, ws):
    qu = [mx_ref.quantize(u[r]) for r in range(N)]
    lay = [pk(wc[r], ws[r]) for r in range(N)]
    link = [[ext(gentries(k[r])) for k in (up, lf, rt)] for r in range(N)]
    now = [x[r] for r in range(N)]
    for step in STEP:
        t, par, z = [], [], []
        for r in range(N):
            q = mx_ref.quantize(now[r])
            link[r] = rotated(mx_ref.matmul(qu[r], q)[::16] + np.float32(0.0), *link[r])
            p = link[r][0][:, :C]
            a = np.where(p == C, np.arange(C), p)
            t.append(decode(q))
            par.append(a)
            m = t[r].astype(BF)
            z.append(mx_ref.quantize(((gcols(m, a).astype(np.float32) + gcols(m, at(a, a)).astype(np.float32)) * np.float32(0.5)).astype(BF)))
        for r in range(N):
            now[r] = tile([gpick(mx_ref.matmul(pick(lay[r], np.arange(128 * b, 128 * b + 128)), z[(r - step) % N]) * np.float32(0.03125), par[r]) + t[r][:, b::4] for b in range(4)])
    y, tr = np.zeros((N, 128, C), np.float32), np.zeros((N, 8, 3 * C), np.float32)
    oc, osc = np.zeros((N, 128, 4 * C), np.uint8), np.zeros((N, 16, C), np.uint8)
    for r in range(N):
        q = mx_ref.quantize(now[r])
        y[r] = mx_ref.matmul(mx_ref.quantize(v[r]), q)
        tr[r] = np.concatenate([k[:, :C] for k in link[r]], axis=1)
        oc[r], osc[r] = emit(q)
    return {"y": y, "tr": tr, "oc": oc, "osc": osc}

@@ -1,0 +1,552 @@
+from concourse.mybir import dt, AluOpType, ActivationFunctionType
+
+C = 384
+H = C // 2
+STEP = [1, 2, 4]
+BIG = 2.0 ** 90
+J0 = 8176.0 * 256
+U = 2.0 ** -12
+F32, BF, U16, I32, X4, U8 = "float32", "bfloat16", "uint16", "int32", "float8_e4m3fn_x4", "uint8"
+
+
+def _sb(n, d):
+    return ("sbuf", [128, n], d)
+
+
+SCRATCH = {
+    "xin": _sb(4 * C, BF), "ut": _sb(512, BF), "vt": _sb(512, BF), "et": _sb(2048, BF),
+    "upt": _sb(24, I32), "lft": _sb(24, I32), "rtt": _sb(24, I32),
+    "uq": _sb(128, X4), "us": _sb(128, U8), "vq": _sb(128, X4), "vs8": _sb(128, U8),
+    "eq": _sb(512, X4), "es": _sb(512, U8), "wq": _sb(512, X4), "wsc": _sb(512, U8),
+    "ml": _sb(6, U16),
+    "cvi": _sb(224, F32), "cai": _sb(128, F32), "xs": _sb(80, F32),
+    "cva0": _sb(224, F32), "cva1": _sb(224, F32), "caa": _sb(128, F32),
+    "cvl": _sb(224, F32), "cal": _sb(128, F32),
+    "wrow": _sb(400, F32), "ra": _sb(C, F32), "rl": _sb(C, F32), "rr": _sb(C, F32),
+    "tbw": _sb(C, F32), "tba": _sb(C, F32), "tbl": _sb(C, F32), "tbr": _sb(C, F32),
+    "td": _sb(C, F32), "drow": _sb(400, F32), "dl": _sb(C, F32), "dr": _sb(C, F32), "tb2": _sb(2 * C, F32),
+    "tk": _sb(2 * C, BF), "krow": _sb(400, BF), "k4row": _sb(C, BF),
+    "r3q": _sb(C, BF), "r3l": _sb(C, BF), "r3r": _sb(C, BF), "r3w": _sb(C, BF), "t3": _sb(4 * C, BF),
+    "te": _sb(C, F32), "erow": _sb(400, F32), "el": _sb(C, F32), "er": _sb(C, F32),
+    "g1": _sb(C, F32), "g2": _sb(C, F32), "g3": _sb(C, F32), "trow": _sb(C, F32),
+    "tel": _sb(2 * C, F32), "tg": _sb(3 * C, F32), "tz": _sb(C, F32), "vg": _sb(C, F32),
+    "fo": _sb(4 * C, BF), "zf": _sb(4 * C, BF), "zk": _sb(4 * C, BF), "zg": _sb(3 * C, BF), "zh": _sb(C, BF), "zt": _sb(4 * C, BF), "zq": _sb(C, X4), "zs": _sb(C, U8),
+    "rs": _sb(4 * C, F32), "xt": _sb(4 * C, BF), "yo": _sb(C, F32),
+}
+_FLOATS = {"n": 72, "m1": 24, "m2": 24, "pp": 72, "pq": 72, "hh": 24, "ee": 24, "j1": 72, "jt": 72, "s3": 72, "yq": 48, "fy": 48, "yp": 48,
+           "yb": 24, "ba": 24, "fv": 48, "pv": 48, "ph": 24, "cy": 48, "cvc": 48, "dy": 48, "dvc": 48, "dsy": 48, "lk": 48, "p1": 24,
+           "ct": 288, "sa": 72, "w1": 48, "w2": 48, "w3": 48, "w4": 48, "w5": 48, "w6": 48, "w7": 48, "w8": 48, "w9": 48, "x2": 48, "jw": 24, "j0": 24, "mt": 32}
+_WHOLES = {"kj": 48, "qi": 24, "vc": 48, "r12": 48, "alr": 48, "ai0": 24, "ai1": 24, "pi": 24, "pb": 24, "pc": 24, "p31": 24, "p15": 24,
+           "pe": 24, "po": 24}
+PIECE = {}
+for _n, _d, _w in (("floats", F32, _FLOATS), ("wholes", I32, _WHOLES)):
+    _at = 0
+    for _k in _w:
+        PIECE[_k] = (_n, _at, _w[_k])
+        _at += _w[_k]
+    SCRATCH[_n] = _sb(_at, _d)
+for _t in range(4):
+    SCRATCH["q%d" % _t] = _sb(C, X4)
+    SCRATCH["qs%d" % _t] = _sb(C, U8)
+    SCRATCH["oa%d" % _t] = _sb(32, U16)
+for _t in range(3):
+    SCRATCH["lq%d" % _t] = _sb(C, X4)
+    SCRATCH["ls%d" % _t] = _sb(C, U8)
+    SCRATCH["ll%d" % _t] = _sb(24, U16)
+SCRATCH["ol"] = _sb(80, U16)
+for _i in range(8):
+    SCRATCH["ps%d" % _i] = ("psum", [128, 512], F32)
+SEMAPHORES = ["sv", "ss", "st", "sg", "ix0", "ix1", "iu", "iv", "ip", "il", "ir", "iw", "iz", "out", "loc",
+              "rq0", "rq1", "rq2", "rl0", "rl1", "rl2"]
+
+
+def rank_program(g, core, T, topo):
+    rank = T.rank_of(core)
+    if rank is None:
+        return
+    A = AluOpType
+    COPY = ActivationFunctionType.Copy
+    N = len(T.cores)
+    queues = {"v": g.vector, "s": g.scalar, "t": g.tensor, "g": g, "y": g.sync}
+    own = {"v": "sv", "s": "ss", "t": "st", "g": "sg"}
+    count = {k: 0 for k in SEMAPHORES}
+    known = {k: {} for k in queues}
+    after = {}
+    seen = {}
+
+    def join(a, b):
+        for k, v in b.items():
+            if a.get(k, 0) < v:
+                a[k] = v
+
+    def W(name, a=0, b=None, step=1):
+        if b is None:
+            b = PIECE[name][2] if name in PIECE else SCRATCH[name][1][1]
+        return (name, a, b, step)
+
+    def S16(name, k, a=0, b=C):
+        return (name, a + k, b, 16)
+
+    def ap(v):
+        name, at = PIECE[v[0]][:2] if v[0] in PIECE else (v[0], 0)
+        return T[name][:, at + v[1]:at + v[2]] if v[3] == 1 else T[name][:, at + v[1]:at + v[2]:v[3]]
+
+    def over(a, b):
+        if a[0][:2] == "ps":
+            return True
+        if a[1] >= b[2] or b[1] >= a[2]:
+            return False
+        return not (a[3] == b[3] and a[3] > 1 and (a[1] - b[1]) % a[3] != 0)
+
+    def waits(qn, reads, writes):
+        need = {}
+        for v, w in [(v, False) for v in reads] + [(v, True) for v in writes]:
+            for o, ow, oq, sem, val in seen.get(v[0], []):
+                if not over(o, v):
+                    continue
+                if not (w or ow) and not (v[0][:2] == "ps" and oq != qn):
+                    continue
+                need[sem] = max(need.get(sem, 0), val)
+        for sem in sorted(need, key=lambda k: -need[k]):
+            if known[qn].get(sem, 0) < need[sem]:
+                queues[qn].wait_ge(T.sem[sem], need[sem])
+                join(known[qn], after.get((sem, need[sem]), {}))
+                join(known[qn], {sem: need[sem]})
+
+    def emit(qn, call, reads, writes):
+        waits(qn, reads, writes)
+        sem = own[qn]
+        count[sem] += 1
+        call().then_inc(T.sem[sem], 1)
+        k = dict(known[qn])
+        k[sem] = count[sem]
+        join(k, after.get((sem, count[sem] - 1), {}))
+        after[(sem, count[sem])] = k
+        for v, w in [(v, False) for v in reads] + [(v, True) for v in writes]:
+            seen.setdefault(v[0], []).append((v, w, qn, sem, count[sem]))
+
+    def load(qn, dst, out, src, sem):
+        count[sem] += 16
+        queues[qn].dma_start(out, src).then_inc(T.sem[sem], 16)
+        seen.setdefault(dst[0], []).append((dst, True, "dma", sem, count[sem]))
+
+    def store(qn, out, src, src_ap):
+        waits(qn, [src], [])
+        count["out"] += 16
+        queues[qn].dma_start(out, src_ap).then_inc(T.sem["out"], 16)
+
+    def tt(out, a, b, op):
+        emit("v", lambda: g.vector.tensor_tensor(ap(out), ap(a), ap(b), op), [a, b], [out])
+
+    def tti(out, win, off, b, op):
+        emit("v", lambda: g.vector.tensor_tensor(ap(out), ap(win).indirect(ap(off)), ap(b), op), [win, off, b], [out])
+
+    def ts(out, a, s1, s2, op0, op1=None):
+        if op1 is None:
+            emit("v", lambda: g.vector.tensor_scalar(ap(out), ap(a), s1, None, op0), [a], [out])
+        else:
+            emit("v", lambda: g.vector.tensor_scalar(ap(out), ap(a), s1, s2, op0, op1), [a], [out])
+
+    def cp(out, a):
+        emit("v", lambda: g.vector.tensor_copy(ap(out), ap(a)), [a], [out])
+
+    def cpi(out, win, off):
+        emit("v", lambda: g.vector.tensor_copy(ap(out), ap(win).indirect(ap(off))), [win, off], [out])
+
+    def tr(out, a):
+        emit("v", lambda: g.vector.transpose(ap(out), ap(a)), [a], [out])
+
+    def fill(out, c):
+        emit("v", lambda: g.vector.memset(ap(out), c), [], [out])
+
+    def quant(q, s, a):
+        emit("v", lambda: g.vector.quantize_mx(ap(q), ap(s), ap(a)), [a], [q, s])
+
+    def act(out, a, scale=1.0, bias=0.0):
+        emit("s", lambda: g.scalar.activation(ap(out), ap(a), COPY, bias=bias, scale=scale), [a], [out])
+
+    def acti(out, win, off, scale=1.0):
+        emit("s", lambda: g.scalar.activation(ap(out), ap(win).indirect(ap(off)), COPY, scale=scale), [win, off], [out])
+
+    def mm(bank, n, lq, lsc, rq, rsc):
+        o = W("ps%d" % bank, 0, n)
+        emit("t", lambda: g.tensor.matmul_mx(ap(o), ap(lq), ap(lsc), ap(rq), ap(rsc), True, True), [lq, lsc, rq, rsc], [o])
+
+    def iota(out, pattern, cm):
+        if out[0] in _WHOLES:
+            emit("g", lambda: g.iota(ap(out), pattern, 0, cm), [], [out])
+        else:
+            emit("g", lambda: g.iota(ap(out), pattern, 0, cm, allow_small_or_imprecise_dtypes=True), [], [out])
+
+    def turn(cv, ca, k, n, out):
+        tr(W(ca, 16, 16 + 32 * k), W(cv, 0, 32 * k))
+        tr(W(cv, 96, 128 + 32 * k), W(ca, 0, 32 * k + 32))
+        cpi(W(out, 0, 16 * n), W(cv, 0, 128 + 32 * k), W("ml", 0, n))
+
+    def half(name, i):
+        return W(name, H * i, H * i + H)
+
+    load("y", W("xin", 0, 4 * H), T.xin[:, 0:4 * H], T.x[:, 0:4 * H], "ix0")
+    load("s", W("upt"), T.upt[:], T.up[:], "ip")
+    load("s", W("lft"), T.lft[:], T.lf[:], "il")
+    load("s", W("rtt"), T.rtt[:], T.rt[:], "ir")
+    load("y", W("xin", 4 * H, 4 * C), T.xin[:, 4 * H:4 * C], T.x[:, 4 * H:4 * C], "ix1")
+    load("s", W("ut"), T.ut[:], T.u[:], "iu")
+    load("y", W("wq"), T.wq[:, 0:512].bitcast(dt.uint8), T.wc[:, 0:2048], "iw")
+    load("y", W("wsc"), T.wsc[:, 0:512], T.ws[:, 0:512], "iz")
+    load("y", W("vt"), T.vt[:], T.v[:], "iv")
+
+    iota(W("pi"), [[0, 24]], 1)
+    iota(W("pb"), [[32, 12], [0, 2]], 0)
+    iota(W("pc"), [[16, 24]], 0)
+    iota(W("te"), [[0, C]], 0)
+    fill(W("et", 0, 512), 1.0)
+    emit("g", lambda: g.affine_select(T.et[:, 0:512], T.et[:, 0:512], [[-1, 512]], A.is_equal, 0.0, 0, 4), [W("et", 0, 512)], [W("et", 0, 512)])
+    for b in ("cvl", "cal", "td", "caa", "cva0", "cva1"):
+        iota(W(b), [[0, SCRATCH[b][1][1]]], 0)
+    for b in range(1, 4):
+        fill(W("et", 512 * b, 512 * b + b), 0.0)
+    fill(W("cvi"), 0.0)
+    fill(W("cai"), 0.0)
+    ts(W("p31"), W("pi"), 31, None, A.bitwise_and)
+    ts(W("p15"), W("pi"), 15, None, A.bitwise_and)
+    ts(W("pe"), W("pi"), 4, 1, A.logical_shift_right, A.bitwise_and)
+    ts(W("po"), W("pi"), 1, None, A.bitwise_and)
+    tt(W("x2", 0, 24), W("p31"), W("pb"), A.add)
+    tt(W("x2", 24, 48), W("p31"), W("pb"), A.add)
+    tt(W("jw"), W("p15"), W("pc"), A.add)
+    tt(W("mt", 0, 6), W("po", 0, 6), W("pe", 0, 6), A.subtract)
+    ts(W("w1", 24, 48), W("jw"), float(C), None, A.subtract)
+    tt(W("mt", 8, 14), W("mt", 0, 6), W("mt", 0, 6), A.mult)
+    ts(W("mt", 0, 6), W("mt", 0, 6), 15.0, None, A.mult)
+    ts(W("mt", 8, 14), W("mt", 8, 14), 112.0, None, A.mult)
+    tt(W("mt", 16, 22), W("mt", 0, 6), W("jw", 0, 6), A.add)
+    tt(W("mt", 24, 30), W("mt", 8, 14), W("mt", 16, 22), A.add)
+    cp(W("ml"), W("mt", 24, 30))
+    fill(W("erow", C, 400), float(C))
+    for b in range(1, 4):
+        act(W("et", 512 * b + b, 512 * b + 512), W("et", 0, 512 - b))
+
+    x1 = W("x2", 0, 24)
+    ts(W("w1", 0, 24), W("upt"), float(C), None, A.is_equal)
+    cp(W("cvi", 24, 48), W("lft"))
+    cp(W("cvi", 48, 72), W("rtt"))
+    tt(W("w2", 0, 24), W("w1", 0, 24), W("w1", 24, 48), A.mult)
+    tt(W("cvi", 0, 24), W("upt"), W("w2", 0, 24), A.add)
+    cp(W("oa0", 0, 24), W("cvi", 0, 24))
+    turn("cvi", "cai", 3, 5, "xs")
+    cp(S16("te", 0), W("xs", 0, 24))
+    cp(S16("te", 1), W("xs", 48, 72))
+    cp(S16("te", 2), W("xs", 24, 48))
+    tr(W("erow", 0, C), W("te"))
+    acti(W("g1"), W("erow"), W("oa0", 0, 24))
+    acti(W("g2"), W("g1"), W("oa0", 0, 24))
+    acti(W("g3"), W("g2"), W("oa0", 0, 24))
+    fill(W("wrow", C, 400), -BIG)
+    fill(W("drow", C, 400), BIG)
+    fill(W("krow", C, 400), 0.0)
+    fill(W("tk"), 0.0)
+    ts(W("j0"), x1, -4096.0, J0, A.mult, A.add)
+    cp(W("jt", 0, 24), W("j0"))
+    cp(W("ai0"), W("xs", 0, 24))
+    cp(W("cvl", 0, 48), W("xs", 24, 72))
+    quant(W("uq"), W("us"), W("ut"))
+    act(W("jt", 24, 72), W("cvl", 0, 48), -4096.0, J0)
+
+    act(W("lk", 0, 24), W("cvl", 0, 24), 1.0, 2 * U)
+    act(W("lk", 24, 48), W("cvl", 24, 48), 1.0, U)
+
+    def tg(i, k):
+        return S16("tg", k, C * i, C * i + C)
+
+    def sides(out, i, who):
+        tt(W("w1", 0, 24), tg(i, 2), who, A.is_equal)
+        tt(W("w1", 24, 48), tg(i, 1), who, A.is_equal)
+        tt(W("w2", 0, 24), W("w1", 0, 24), W("w1", 24, 48), A.add)
+        tt(W("w2", 24, 48), W("w2", 0, 24), W("w1", 24, 48), A.add)
+        ts(out, W("w2", 24, 48), U, None, A.mult)
+
+    sT, s1, s2 = [W("sa", 24 * i, 24 * i + 24) for i in range(3)]
+
+    def ct(i):
+        return W("ct", 24 * i, 24 * i + 24)
+
+    def own_shapes():
+        act(W("s3", 0, 24), sT, 256.0 / U)
+        act(W("s3", 24, 48), sT, 768.0 / U, 256.0)
+        act(W("s3", 48, 72), sT, 768.0 / U, 512.0)
+        act(W("cy", 0, 24), sT, 768.0 / U, 4352.0)
+        act(W("cy", 24, 48), sT, 768.0 / U, 8704.0)
+        act(ct(0), sT, 272.0 / U)
+        act(W("dsy", 0, 24), sT, -1.0 / U, 2.0)
+        act(W("dsy", 24, 48), sT, -1.0 / U, 1.0)
+
+    def upper_shapes():
+        act(ct(1), s1, 48.0 / U)
+        act(ct(2), s1, 17.0 / U)
+        act(ct(3), s2, 3.0 / U)
+
+    def targets(p1, p):
+        tt(W("dy", 0, 24), W("lk", 0, 24), p, A.subtract)
+        tt(W("dy", 24, 48), W("lk", 24, 48), p, A.subtract)
+        tt(ct(4), sT, s1, A.add)
+        tt(ct(6), x1, p1, A.subtract)
+        ts(ct(7), s1, 0.0, None, A.is_equal)
+        tt(W("dvc", 24, 48), p1, p, A.subtract)
+        ts(ct(8), ct(4), 3 * U, 65536.0, A.not_equal, A.mult)
+        tt(ct(9), ct(7), ct(6), A.mult)
+        tt(W("cvc", 0, 24), ct(0), ct(1), A.add)
+        tt(ct(10), ct(2), ct(3), A.add)
+        tt(W("dvc", 0, 24), ct(9), W("dvc", 24, 48), A.add)
+        tt(W("cvc", 24, 48), ct(10), ct(8), A.add)
+
+    for i in range(2):
+        quant(half("q0", i), half("qs0", i), W("xin", 4 * H * i, 4 * H * i + 4 * H))
+    tr(W("tg", 0, C), W("g1"))
+    cp(W("cvl", 48, 72), tg(0, 0))
+    turn("cvl", "cal", 3, 5, "ol")
+
+    me = T.cores
+    eight = min(len(topo.engines(core, d)) for d in me if d != core)
+
+    def send(dst, out, src, sem, reads):
+        waits("g", reads, [])
+        rid, pid, _ = topo.addr(dst)
+        e = topo.engines(core, dst)[:eight]
+        g.remote_dma(out, src, T.sem[sem], T.sem["loc"], pid, rid, sum(1 << i for i in e))
+        count["loc"] += len(e)
+
+    def arrive(sem, total, names):
+        for b in names:
+            seen.setdefault(b, []).append((W(b), True, "far", sem, total))
+
+    def col(n, b):
+        return W(n, C * b, C * b + C)
+
+    for t in range(3):
+        q, qs, lq, ls, ll = "q%d" % t, "qs%d" % t, "lq%d" % t, "ls%d" % t, "ll%d" % t
+        oa, on = W("oa%d" % t, 0, 24), "oa%d" % (t + 1)
+        dst = me[(rank + STEP[t]) % N]
+        send(dst, ap(W(lq)).bitcast(dt.uint8), ap(W(q)).bitcast(dt.uint8), "rq%d" % t, [W(q)])
+        send(dst, ap(W(ls)), ap(W(qs)), "rq%d" % t, [W(qs)])
+        arrive("rq%d" % t, 2 * eight, [lq, ls])
+        arrive("rl%d" % t, eight, [ll])
+        a = W("cva%d" % (t % 2), 0, 24)
+        an = W("cva%d" % ((t + 1) % 2), 0, 24)
+        aL, aR, aAA = W("ol", 0, 24), W("ol", 24, 48), W("ol", 48, 72)
+        for i in range(2):
+            mm(i, H, W("uq"), W("us"), half(q, i), half(qs, i))
+            mm(6 + i, H, W("uq"), W("us"), half(q, i), half(qs, i))
+        for i in range(2):
+            act(half("wrow", i), W("ps%d" % i, 0, H))
+        for i in range(2):
+            tr(half("tbw", i), W("ps%d" % (6 + i), 0, H))
+        if t == 0:
+            quant(W("eq"), W("es"), W("et"))
+        fb = [0, 1, 6]
+        for b in range(3):
+            mm(fb[b], C, W("eq", 128 * b, 128 * b + 128), W("es", 128 * b, 128 * b + 128), W(q), W(qs))
+        acti(W("ra"), W("wrow"), oa)
+        acti(W("rl"), W("wrow"), aL)
+        acti(W("rr"), W("wrow"), aR)
+        if t == 0:
+            sides(sT, 0, x1)
+            own_shapes()
+            tt(a, W("ai0"), sT, A.add)
+            tr(W("tg", C, 2 * C), W("g2"))
+            tr(W("tg", 2 * C, 3 * C), W("g3"))
+        else:
+            act(W("jt", 24, 72), lr, -4096.0, J0)
+            act(W("lk", 0, 24), W("cvl", 0, 24), 1.0, 2 * U)
+            act(W("lk", 24, 48), W("cvl", 24, 48), 1.0, U)
+            act(S16("te", 1), W("cvl", 24, 48))
+            act(S16("te", 2), W("cvl", 0, 24))
+            upper_shapes()
+        tr(W("tba"), W("ra"))
+        w0 = S16("tbw", 0)
+        tt(W("n", 0, 24), S16("tba", 0), w0, A.subtract)
+        tr(W("tbl"), W("rl"))
+        tt(W("n", 24, 48), w0, S16("tbl", 0), A.subtract)
+        tt(W("j1"), W("jt"), W("s3"), A.add)
+        tr(W("tbr"), W("rr"))
+        tt(W("m1"), W("n", 0, 24), W("n", 24, 48), A.min)
+        tt(W("n", 48, 72), w0, S16("tbr", 0), A.subtract)
+        for b in range(2):
+            act(col("fo", b), W("ps%d" % fb[b], 0, C))
+        M = S16("td", 0)
+        tt(M, W("m1"), W("n", 48, 72), A.min)
+        for i in range(3):
+            tt(W("pp", 24 * i, 24 * i + 24), W("n", 24 * i, 24 * i + 24), M, A.is_le)
+        tt(W("pq"), W("pp"), W("j1"), A.mult)
+        tt(W("hh"), W("pq", 0, 24), W("pq", 24, 48), A.max)
+        tt(S16("td", 1), W("hh"), W("pq", 48, 72), A.max)
+        tr(W("drow", 0, C), W("td"))
+        acti(W("dl"), W("drow"), aL)
+        acti(W("dr"), W("drow"), aR)
+        act(col("fo", 2), W("ps%d" % fb[2], 0, C))
+        if t == 0:
+            sides(s1, 1, W("ai0"))
+            sides(s2, 2, W("cvl", 48, 72))
+            tt(W("p1"), W("cvl", 48, 72), s1, A.add)
+            upper_shapes()
+            targets(W("p1"), a)
+        else:
+            targets(tg(0, 0), a)
+        tr(W("tb2", 0, C), W("dl"))
+        nl, nr = S16("tb2", 0), S16("tb2", 0, C, 2 * C)
+        tt(W("m1"), W("n", 0, 24), nl, A.min)
+        tr(W("tb2", C, 2 * C), W("dr"))
+        tt(W("m2"), W("m1"), nr, A.min)
+        tt(W("pp", 24, 48), nl, W("m2"), A.is_le)
+        tt(W("pp", 48, 72), nr, W("m2"), A.is_le)
+        tt(W("pp", 0, 24), W("n", 0, 24), W("m2"), A.is_le)
+        tt(W("pq", 24, 72), W("pp", 24, 72), S16("tb2", 1, 0, 2 * C), A.mult)
+        tt(W("pq", 0, 24), W("pp", 0, 24), W("j0"), A.mult)
+        tt(W("hh"), W("pq", 24, 48), W("pq", 48, 72), A.max)
+        ts(W("ee"), W("m2"), 0.0, 3840.0, A.is_ge, A.mult)
+        tt(W("kj", 0, 24), W("hh"), W("pq", 0, 24), A.max)
+        ts(W("kj", 24, 48), W("kj", 0, 24), 0xF00, None, A.bitwise_and)
+        tt(S16("tk", 0), W("kj", 24, 48), W("ee"), A.max)
+        tr(W("krow", 0, C), W("tk", 0, C))
+        ts(S16("tk", 0, C, 2 * C), S16("tk", 0), 16.0, None, A.mult)
+        tr(W("k4row"), W("tk", C, 2 * C))
+        acti(W("r3l"), W("krow"), aL, 1.0 / 256)
+        acti(W("r3r"), W("krow"), aR, 1.0 / 256)
+        tti(W("r3q"), W("krow"), oa, W("k4row"), A.add)
+        acti(W("r3w"), W("r3q"), aAA, 1.0 / 256)
+        tr(W("t3", 0, C), W("r3q"))
+        tr(W("t3", C, 2 * C), W("r3l"))
+        tr(W("t3", 2 * C, 3 * C), W("r3r"))
+        q2 = S16("t3", 0, 0, C)
+        tt(W("yq", 0, 24), S16("t3", 0, C, 2 * C), q2, A.add)
+        tt(W("yq", 24, 48), S16("t3", 0, 2 * C, 3 * C), q2, A.add)
+        tt(W("fy"), W("yq"), W("cy"), A.is_equal)
+        tt(W("yp"), W("fy"), W("dy"), A.mult)
+        tt(W("yb"), W("yp", 0, 24), W("yp", 24, 48), A.add)
+        tt(W("ba"), W("yb"), a, A.add)
+        tr(W("t3", 3 * C, 4 * C), W("r3w"))
+        tt(W("qi"), S16("t3", 0, 3 * C, 4 * C), q2, A.add)
+        ts(W("vc", 0, 24), W("qi"), 0xFFF0, None, A.bitwise_and)
+        ts(W("vc", 24, 48), W("qi"), 0x0FFF, None, A.bitwise_and)
+        tt(W("fv"), W("vc"), W("cvc"), A.is_equal)
+        tt(W("pv"), W("fv"), W("dvc"), A.mult)
+        tt(W("ph"), W("pv", 0, 24), W("pv", 24, 48), A.add)
+        tt(an, W("ph"), W("ba"), A.add)
+        turn(an[0], "caa", 1, 2, on)
+        send(dst, ap(W(ll)), ap(W(on, 0, 24)), "rl%d" % t, [W(on)])
+        oan = W(on, 0, 24)
+
+        for b in range(4):
+            mm(2 + b, C, W("eq", 128 * b, 128 * b + 128), W("es", 128 * b, 128 * b + 128), W(lq), W(ls))
+        for b in range(4):
+            act(col("zf", b), W("ps%d" % (2 + b), 0, C), 0.5)
+
+        ao, ai = W("ai%d" % (t % 2)), W("ai%d" % ((t + 1) % 2))
+        cp(S16("te", 0), an)
+        cp(ai, an)
+        tr(W("erow", 0, C), W("te"))
+        acti(W("el"), W("erow"), aL)
+        acti(W("er"), W("erow"), aR)
+        if t < 2:
+            tt(sT, an, ai, A.subtract)
+        tt(W("w3", 0, 24), W("fv", 0, 24), W("dsy", 24, 48), A.mult)
+        tt(W("w3", 24, 48), W("fv", 0, 24), W("dsy", 0, 24), A.mult)
+        for b in range(3):
+            cp(col("zg", b), col("zf", b))
+        tr(W("tel", 0, C), W("el"))
+        tr(W("tel", C, 2 * C), W("er"))
+
+        off = W(ll)
+        acti(col("zk", 3), col("zf", 3), off)
+        for b in range(3):
+            tti(col("zk", b), col("zf", b), off, col("zg", b), A.add)
+            if b == 1:
+                cp(W("zh"), col("zk", 3))
+            if b < 2:
+                acti(W("zt", b, 4 * C, 4), col("zk", b), off)
+        for i in range(2):
+            oh = W(ll, 12 * i, 12 * i + 12)
+            acti(W("zt", 4 * H * i + 2, 4 * H * i + 4 * H, 4), col("zk", 2), oh)
+            tti(W("zt", 4 * H * i + 3, 4 * H * i + 4 * H, 4), col("zk", 3), oh, half("zh", i), A.add)
+        if t < 2:
+            own_shapes()
+        rb = [[2, 3, 4, 5], [6, 7, 0, 1]]
+        for i in range(2):
+            quant(half("zq", i), half("zs", i), W("zt", 4 * H * i, 4 * H * i + 4 * H))
+
+        for b in range(4):
+            for i in range(2):
+                mm(rb[i][b], H, W("wq", 128 * b, 128 * b + 128), W("wsc", 128 * b, 128 * b + 128), half("zq", i), half("zs", i))
+        for b in range(4):
+            for i in range(2):
+                act(W("rs", C * b + H * i, C * b + H * i + H), W("ps%d" % rb[i][b], 0, H), 0.03125)
+
+        lr = W("cvl", 0, 48)
+        cp(W("alr"), S16("tel", 0, 0, 2 * C))
+        tt(W("w1"), W("alr"), W("x2"), A.not_equal)
+        tt(W("w2"), W("alr"), lr, A.subtract)
+        tt(W("w4"), W("w1"), W("w2"), A.mult)
+        tt(W("w5"), lr, W("w4"), A.add)
+        acti(W("vg"), col("rs", 3), oan)
+        mm(2, C, W("eq", 384, 512), W("es", 384, 512), W(q), W(qs))
+
+        def children(part):
+            if part == 0:
+                tt(W("w1", 0, 24), S16("tel", 1), W("w5", 0, 24), A.subtract)
+                tt(W("w1", 24, 48), S16("tel", 2, C, 2 * C), W("w5", 24, 48), A.subtract)
+                tt(W("w2", 0, 24), W("w5", 0, 24), ao, A.subtract)
+                tt(W("w2", 24, 48), ao, W("w5", 24, 48), A.subtract)
+                return
+            tt(W("w4"), W("fy"), W("w1"), A.mult)
+            tt(W("w6"), W("w3"), W("w2"), A.mult)
+            tt(W("w7"), W("w5"), W("w4"), A.add)
+            tt(lr, W("w7"), W("w6"), A.add)
+        if t < 2:
+            acti(W("g1"), W("erow"), oan)
+            acti(W("g2"), W("g1"), oan)
+        else:
+            children(0)
+            children(1)
+            fill(W("tz"), 0.0)
+            tt(W("w1", 0, 24), ai, x1, A.is_equal)
+            ts(W("w1", 24, 48), ai, -1.0, float(C), A.mult, A.add)
+            cp(S16("tz", 1), W("cvl", 0, 24))
+            cp(S16("tz", 2), W("cvl", 24, 48))
+            tt(W("w4", 0, 24), W("w1", 0, 24), W("w1", 24, 48), A.mult)
+            tt(S16("tz", 0), ai, W("w4", 0, 24), A.add)
+            tr(W("trow"), W("tz"))
+            for i in range(3):
+                store("y", T.tr[:, C * i:C * i + C], W("trow"), T.trow[i:128:16, 0:C])
+            quant(W("vq"), W("vs8"), W("vt"))
+
+        for b in range(3):
+            tti(W("xt", b, 4 * C, 4), col("rs", b), oan, col("fo", b), A.add)
+        if t < 2:
+            children(0)
+        for i in range(2):
+            tt(W("xt", 4 * H * i + 3, 4 * H * i + 4 * H, 4), half("vg", i), W("ps2", H * i, H * i + H), A.add)
+            quant(half("q%d" % (t + 1), i), half("qs%d" % (t + 1), i), W("xt", 4 * H * i, 4 * H * i + 4 * H))
+        if t < 2:
+            children(1)
+            tr(W("tg", 0, C), W("g1"))
+            cp(W("cvl", 48, 72), tg(0, 0))
+            turn("cvl", "cal", 3, 5, "ol")
+            tr(W("tg", C, 2 * C), W("g2"))
+            cp(W("r12"), S16("tg", 0, 0, 2 * C))
+            tt(W("sa", 24, 72), S16("tg", 0, 0, 2 * C), W("r12"), A.subtract)
+
+    for i in range(2):
+        mm(i, H, W("vq"), W("vs8"), half("q3", i), half("qs3", i))
+    store("y", T.oc[:], W("q3"), T.q3[:, 0:C].bitcast(dt.uint8))
+    act(half("yo", 0), W("ps0", 0, H))
+    cp(half("yo", 1), W("ps1", 0, H))
+    store("s", T.y[:, 0:H], half("yo", 0), T.yo[:, 0:H])
+    store("y", T.y[:, H:C], half("yo", 1), T.yo[:, H:C])
+    for k in range(4):
+        store("y" if k % 2 else "s", T.osc[4 * k:4 * k + 4, 0:C], W("qs3"), T.qs3[32 * k:32 * k + 4, 0:C])
+    for t in range(3):
+        count["rq%d" % t] = 2 * eight
+        count["rl%d" % t] = eight
+    for sem in SEMAPHORES:
+        if known["g"].get(sem, 0) < count[sem]:
+            g.wait_ge(T.sem[sem], count[sem])

@@ -26,7 +26,7 @@ SCRATCH = {
     "tbw": _sb(C, F32), "tba": _sb(C, F32), "tbl": _sb(C, F32), "tbr": _sb(C, F32),
     "td": _sb(C, F32), "drow": _sb(400, F32), "dl": _sb(C, F32), "dr": _sb(C, F32), "tb2": _sb(2 * C, F32),
     "tk": _sb(2 * C, BF), "krow": _sb(400, BF), "k4row": _sb(C, BF),
-    "r3q": _sb(C, BF), "r3l": _sb(C, BF), "r3r": _sb(C, BF), "r3w": _sb(C, BF), "t3": _sb(4 * C, BF),
+    "r3q": _sb(C, BF), "r3lr": _sb(2 * C, BF), "r3w": _sb(C, BF), "t3": _sb(4 * C, BF),
     "te": _sb(C, F32), "erow": _sb(400, F32), "el": _sb(C, F32), "er": _sb(C, F32),
     "g1": _sb(C, F32), "g2": _sb(C, F32), "g3": _sb(C, F32), "trow": _sb(C, F32),
     "tel": _sb(2 * C, F32), "tg": _sb(3 * C, F32), "tz": _sb(C, F32), "vg": _sb(C, F32),
@@ -180,8 +180,16 @@ def rank_program(g, core, T, topo):
 
     def turn(cv, ca, k, n, out):
         tr(W(ca, 16, 16 + 32 * k), W(cv, 0, 32 * k))
+        spare(1)
         tr(W(cv, 96, 128 + 32 * k), W(ca, 0, 32 * k + 32))
+        spare(1)
         cpi(W(out, 0, 16 * n), W(cv, 0, 128 + 32 * k), W("ml", 0, n))
+
+    todo = []
+
+    def spare(n):
+        for _ in range(min(n, len(todo))):
+            todo.pop(0)()
 
     def half(name, i):
         return W(name, H * i, H * i + H)
@@ -199,10 +207,9 @@ def rank_program(g, core, T, topo):
     iota(W("pi"), [[0, 24]], 1)
     iota(W("pb"), [[32, 12], [0, 2]], 0)
     iota(W("pc"), [[16, 24]], 0)
-    iota(W("te"), [[0, C]], 0)
     fill(W("et", 0, 512), 1.0)
     emit("g", lambda: g.affine_select(T.et[:, 0:512], T.et[:, 0:512], [[-1, 512]], A.is_equal, 0.0, 0, 4), [W("et", 0, 512)], [W("et", 0, 512)])
-    for b in ("cvl", "cal", "td", "caa", "cva0", "cva1"):
+    for b in ("te", "cvl", "cal", "td", "cva0"):
         iota(W(b), [[0, SCRATCH[b][1][1]]], 0)
     for b in range(1, 4):
         fill(W("et", 512 * b, 512 * b + b), 0.0)
@@ -240,21 +247,9 @@ def rank_program(g, core, T, topo):
     cp(S16("te", 2), W("xs", 24, 48))
     tr(W("erow", 0, C), W("te"))
     acti(W("g1"), W("erow"), W("oa0", 0, 24))
-    acti(W("g2"), W("g1"), W("oa0", 0, 24))
-    acti(W("g3"), W("g2"), W("oa0", 0, 24))
     fill(W("wrow", C, 400), -BIG)
-    fill(W("drow", C, 400), BIG)
-    fill(W("krow", C, 400), 0.0)
-    fill(W("tk"), 0.0)
-    ts(W("j0"), x1, -4096.0, J0, A.mult, A.add)
-    cp(W("jt", 0, 24), W("j0"))
-    cp(W("ai0"), W("xs", 0, 24))
     cp(W("cvl", 0, 48), W("xs", 24, 72))
     quant(W("uq"), W("us"), W("ut"))
-    act(W("jt", 24, 72), W("cvl", 0, 48), -4096.0, J0)
-
-    act(W("lk", 0, 24), W("cvl", 0, 24), 1.0, 2 * U)
-    act(W("lk", 24, 48), W("cvl", 24, 48), 1.0, U)
 
     def tg(i, k):
         return S16("tg", k, C * i, C * i + C)
@@ -287,18 +282,19 @@ def rank_program(g, core, T, topo):
         act(ct(3), s2, 3.0 / U)
 
     def targets(p1, p):
-        tt(W("dy", 0, 24), W("lk", 0, 24), p, A.subtract)
-        tt(W("dy", 24, 48), W("lk", 24, 48), p, A.subtract)
-        tt(ct(4), sT, s1, A.add)
-        tt(ct(6), x1, p1, A.subtract)
-        ts(ct(7), s1, 0.0, None, A.is_equal)
-        tt(W("dvc", 24, 48), p1, p, A.subtract)
-        ts(ct(8), ct(4), 3 * U, 65536.0, A.not_equal, A.mult)
-        tt(ct(9), ct(7), ct(6), A.mult)
-        tt(W("cvc", 0, 24), ct(0), ct(1), A.add)
-        tt(ct(10), ct(2), ct(3), A.add)
-        tt(W("dvc", 0, 24), ct(9), W("dvc", 24, 48), A.add)
-        tt(W("cvc", 24, 48), ct(10), ct(8), A.add)
+        return [
+            lambda: tt(W("dy", 0, 24), W("lk", 0, 24), p, A.subtract),
+            lambda: tt(W("dy", 24, 48), W("lk", 24, 48), p, A.subtract),
+            lambda: tt(ct(4), sT, s1, A.add),
+            lambda: tt(ct(6), x1, p1, A.subtract),
+            lambda: ts(ct(7), s1, 0.0, None, A.is_equal),
+            lambda: ts(ct(8), ct(4), 3 * U, 65536.0, A.not_equal, A.mult),
+            lambda: tt(W("dvc", 24, 48), p1, p, A.subtract),
+            lambda: tt(ct(9), ct(7), ct(6), A.mult),
+            lambda: tt(W("cvc", 0, 24), ct(0), ct(1), A.add),
+            lambda: tt(ct(10), ct(2), ct(3), A.add),
+            lambda: tt(W("dvc", 0, 24), ct(9), W("dvc", 24, 48), A.add),
+            lambda: tt(W("cvc", 24, 48), ct(10), ct(8), A.add)]
 
     for i in range(2):
         quant(half("q0", i), half("qs0", i), W("xin", 4 * H * i, 4 * H * i + 4 * H))
@@ -342,6 +338,13 @@ def rank_program(g, core, T, topo):
         for i in range(2):
             tr(half("tbw", i), W("ps%d" % (6 + i), 0, H))
         if t == 0:
+            for b in ("tk", "caa", "cva1", "tz"):
+                iota(W(b), [[0, SCRATCH[b][1][1]]], 0)
+            fill(W("drow", C, 400), BIG)
+            fill(W("krow", C, 400), 0.0)
+            ts(W("j0"), x1, -4096.0, J0, A.mult, A.add)
+            cp(W("ai0"), W("xs", 0, 24))
+            cp(W("jt", 0, 24), W("j0"))
             quant(W("eq"), W("es"), W("et"))
         fb = [0, 1, 6]
         for b in range(3):
@@ -351,30 +354,29 @@ def rank_program(g, core, T, topo):
         acti(W("rr"), W("wrow"), aR)
         if t == 0:
             sides(sT, 0, x1)
-            own_shapes()
             tt(a, W("ai0"), sT, A.add)
-            tr(W("tg", C, 2 * C), W("g2"))
-            tr(W("tg", 2 * C, 3 * C), W("g3"))
+        own_shapes()
+        act(W("jt", 24, 72), W("cvl", 0, 48), -4096.0, J0)
+        act(W("lk", 0, 24), W("cvl", 0, 24), 1.0, 2 * U)
+        act(W("lk", 24, 48), W("cvl", 24, 48), 1.0, U)
+        acti(W("g2"), W("g1"), oa)
+        if t == 0:
+            acti(W("g3"), W("g2"), oa)
         else:
-            act(W("jt", 24, 72), lr, -4096.0, J0)
-            act(W("lk", 0, 24), W("cvl", 0, 24), 1.0, 2 * U)
-            act(W("lk", 24, 48), W("cvl", 24, 48), 1.0, U)
             act(S16("te", 1), W("cvl", 24, 48))
             act(S16("te", 2), W("cvl", 0, 24))
-            upper_shapes()
         tr(W("tba"), W("ra"))
         w0 = S16("tbw", 0)
         tt(W("n", 0, 24), S16("tba", 0), w0, A.subtract)
         tr(W("tbl"), W("rl"))
         tt(W("n", 24, 48), w0, S16("tbl", 0), A.subtract)
-        tt(W("j1"), W("jt"), W("s3"), A.add)
         tr(W("tbr"), W("rr"))
         tt(W("m1"), W("n", 0, 24), W("n", 24, 48), A.min)
         tt(W("n", 48, 72), w0, S16("tbr", 0), A.subtract)
-        for b in range(2):
-            act(col("fo", b), W("ps%d" % fb[b], 0, C))
+        act(col("fo", 0), W("ps%d" % fb[0], 0, C))
         M = S16("td", 0)
         tt(M, W("m1"), W("n", 48, 72), A.min)
+        tt(W("j1"), W("jt"), W("s3"), A.add)
         for i in range(3):
             tt(W("pp", 24 * i, 24 * i + 24), W("n", 24 * i, 24 * i + 24), M, A.is_le)
         tt(W("pq"), W("pp"), W("j1"), A.mult)
@@ -383,20 +385,27 @@ def rank_program(g, core, T, topo):
         tr(W("drow", 0, C), W("td"))
         acti(W("dl"), W("drow"), aL)
         acti(W("dr"), W("drow"), aR)
-        act(col("fo", 2), W("ps%d" % fb[2], 0, C))
+        for b in range(1, 3):
+            act(col("fo", b), W("ps%d" % fb[b], 0, C))
+        tr(W("tg", C, 2 * C), W("g2"))
         if t == 0:
+            tr(W("tg", 2 * C, 3 * C), W("g3"))
             sides(s1, 1, W("ai0"))
             sides(s2, 2, W("cvl", 48, 72))
             tt(W("p1"), W("cvl", 48, 72), s1, A.add)
-            upper_shapes()
-            targets(W("p1"), a)
         else:
-            targets(tg(0, 0), a)
+            cp(W("r12"), S16("tg", 0, 0, 2 * C))
+            tt(W("sa", 24, 72), S16("tg", 0, 0, 2 * C), W("r12"), A.subtract)
+        upper_shapes()
+        todo.extend(targets(W("p1") if t == 0 else tg(0, 0), a))
+        spare(1)
         tr(W("tb2", 0, C), W("dl"))
         nl, nr = S16("tb2", 0), S16("tb2", 0, C, 2 * C)
         tt(W("m1"), W("n", 0, 24), nl, A.min)
         tr(W("tb2", C, 2 * C), W("dr"))
+        spare(1)
         tt(W("m2"), W("m1"), nr, A.min)
+        spare(1)
         tt(W("pp", 24, 48), nl, W("m2"), A.is_le)
         tt(W("pp", 48, 72), nr, W("m2"), A.is_le)
         tt(W("pp", 0, 24), W("n", 0, 24), W("m2"), A.is_le)
@@ -405,33 +414,46 @@ def rank_program(g, core, T, topo):
         tt(W("hh"), W("pq", 24, 48), W("pq", 48, 72), A.max)
         ts(W("ee"), W("m2"), 0.0, 3840.0, A.is_ge, A.mult)
         tt(W("kj", 0, 24), W("hh"), W("pq", 0, 24), A.max)
+        spare(1)
         ts(W("kj", 24, 48), W("kj", 0, 24), 0xF00, None, A.bitwise_and)
+        spare(1)
         tt(S16("tk", 0), W("kj", 24, 48), W("ee"), A.max)
+        spare(1)
         tr(W("krow", 0, C), W("tk", 0, C))
         ts(S16("tk", 0, C, 2 * C), S16("tk", 0), 16.0, None, A.mult)
+        spare(1)
         tr(W("k4row"), W("tk", C, 2 * C))
-        acti(W("r3l"), W("krow"), aL, 1.0 / 256)
-        acti(W("r3r"), W("krow"), aR, 1.0 / 256)
+        spare(1)
+        acti(W("r3lr"), W("krow"), W("ol", 0, 48), 1.0 / 256)
         tti(W("r3q"), W("krow"), oa, W("k4row"), A.add)
         acti(W("r3w"), W("r3q"), aAA, 1.0 / 256)
+        spare(1)
         tr(W("t3", 0, C), W("r3q"))
-        tr(W("t3", C, 2 * C), W("r3l"))
-        tr(W("t3", 2 * C, 3 * C), W("r3r"))
+        spare(1)
         q2 = S16("t3", 0, 0, C)
+        tr(W("t3", C, 3 * C), W("r3lr"))
+        spare(1)
         tt(W("yq", 0, 24), S16("t3", 0, C, 2 * C), q2, A.add)
         tt(W("yq", 24, 48), S16("t3", 0, 2 * C, 3 * C), q2, A.add)
+        spare(1)
         tt(W("fy"), W("yq"), W("cy"), A.is_equal)
+        spare(1)
         tt(W("yp"), W("fy"), W("dy"), A.mult)
-        tt(W("yb"), W("yp", 0, 24), W("yp", 24, 48), A.add)
-        tt(W("ba"), W("yb"), a, A.add)
         tr(W("t3", 3 * C, 4 * C), W("r3w"))
+        tt(W("hh"), W("yp", 0, 24), W("yp", 24, 48), A.add)
         tt(W("qi"), S16("t3", 0, 3 * C, 4 * C), q2, A.add)
+        tt(W("ba"), W("hh"), a, A.add)
         ts(W("vc", 0, 24), W("qi"), 0xFFF0, None, A.bitwise_and)
         ts(W("vc", 24, 48), W("qi"), 0x0FFF, None, A.bitwise_and)
+        spare(len(todo))
         tt(W("fv"), W("vc"), W("cvc"), A.is_equal)
+        tt(W("yb"), W("fy", 0, 24), W("fy", 24, 48), A.add)
         tt(W("pv"), W("fv"), W("dvc"), A.mult)
+        tt(W("w1", 0, 24), W("yb"), W("fv", 24, 48), A.add)
         tt(W("ph"), W("pv", 0, 24), W("pv", 24, 48), A.add)
         tt(an, W("ph"), W("ba"), A.add)
+        ao, ai = W("ai%d" % (t % 2)), W("ai%d" % ((t + 1) % 2))
+        todo.extend([lambda: cp(ai, an), lambda: cp(S16("te", 0), an)])
         turn(an[0], "caa", 1, 2, on)
         send(dst, ap(W(ll)), ap(W(on, 0, 24)), "rl%d" % t, [W(on)])
         oan = W(on, 0, 24)
@@ -441,14 +463,16 @@ def rank_program(g, core, T, topo):
         for b in range(4):
             act(col("zf", b), W("ps%d" % (2 + b), 0, C), 0.5)
 
-        ao, ai = W("ai%d" % (t % 2)), W("ai%d" % ((t + 1) % 2))
-        cp(S16("te", 0), an)
-        cp(ai, an)
+        tt(W("w1", 24, 48), ai, x1, A.subtract)
+        tt(W("w2", 0, 24), W("w1", 0, 24), W("w1", 24, 48), A.mult)
+        tt(S16("te", 3), W("w2", 0, 24), x1, A.add)
         tr(W("erow", 0, C), W("te"))
         acti(W("el"), W("erow"), aL)
         acti(W("er"), W("erow"), aR)
         if t < 2:
             tt(sT, an, ai, A.subtract)
+        else:
+            quant(W("vq"), W("vs8"), W("vt"))
         tt(W("w3", 0, 24), W("fv", 0, 24), W("dsy", 24, 48), A.mult)
         tt(W("w3", 24, 48), W("fv", 0, 24), W("dsy", 0, 24), A.mult)
         for b in range(3):
@@ -460,16 +484,14 @@ def rank_program(g, core, T, topo):
         acti(col("zk", 3), col("zf", 3), off)
         for b in range(3):
             tti(col("zk", b), col("zf", b), off, col("zg", b), A.add)
-            if b == 1:
-                cp(W("zh"), col("zk", 3))
+            if b == 0:
+                emit("g", lambda: g.affine_select(T.zh[:], T.zk[:, 3 * C:4 * C], [[1, C]], A.is_ge, 0.0, 0, 1), [col("zk", 3)], [W("zh")])
             if b < 2:
                 acti(W("zt", b, 4 * C, 4), col("zk", b), off)
         for i in range(2):
             oh = W(ll, 12 * i, 12 * i + 12)
             acti(W("zt", 4 * H * i + 2, 4 * H * i + 4 * H, 4), col("zk", 2), oh)
             tti(W("zt", 4 * H * i + 3, 4 * H * i + 4 * H, 4), col("zk", 3), oh, half("zh", i), A.add)
-        if t < 2:
-            own_shapes()
         rb = [[2, 3, 4, 5], [6, 7, 0, 1]]
         for i in range(2):
             quant(half("zq", i), half("zs", i), W("zt", 4 * H * i, 4 * H * i + 4 * H))
@@ -482,32 +504,27 @@ def rank_program(g, core, T, topo):
                 act(W("rs", C * b + H * i, C * b + H * i + H), W("ps%d" % rb[i][b], 0, H), 0.03125)
 
         lr = W("cvl", 0, 48)
-        cp(W("alr"), S16("tel", 0, 0, 2 * C))
-        tt(W("w1"), W("alr"), W("x2"), A.not_equal)
-        tt(W("w2"), W("alr"), lr, A.subtract)
-        tt(W("w4"), W("w1"), W("w2"), A.mult)
-        tt(W("w5"), lr, W("w4"), A.add)
-        acti(W("vg"), col("rs", 3), oan)
+        lz, lzl, lzr = S16("tel", 3, 0, 2 * C), S16("tel", 3), S16("tel", 3, C, 2 * C)
+        tt(W("w1", 0, 24), S16("tel", 1), lzl, A.subtract)
+        tt(W("w1", 24, 48), S16("tel", 2, C, 2 * C), lzr, A.subtract)
+        tt(W("w2", 0, 24), lzl, ao, A.subtract)
+        tt(W("w2", 24, 48), ao, lzr, A.subtract)
+        tt(W("w4"), W("fy"), W("w1"), A.mult)
+        tt(W("w6"), W("w3"), W("w2"), A.mult)
+        tt(W("w7"), lz, W("w4"), A.add)
+        tt(lr, W("w7"), W("w6"), A.add)
+        for i in range(2):
+            acti(half("vg", i), col("rs", 3), W(on, 12 * i, 12 * i + 12))
         mm(2, C, W("eq", 384, 512), W("es", 384, 512), W(q), W(qs))
-
-        def children(part):
-            if part == 0:
-                tt(W("w1", 0, 24), S16("tel", 1), W("w5", 0, 24), A.subtract)
-                tt(W("w1", 24, 48), S16("tel", 2, C, 2 * C), W("w5", 24, 48), A.subtract)
-                tt(W("w2", 0, 24), W("w5", 0, 24), ao, A.subtract)
-                tt(W("w2", 24, 48), ao, W("w5", 24, 48), A.subtract)
-                return
-            tt(W("w4"), W("fy"), W("w1"), A.mult)
-            tt(W("w6"), W("w3"), W("w2"), A.mult)
-            tt(W("w7"), W("w5"), W("w4"), A.add)
-            tt(lr, W("w7"), W("w6"), A.add)
         if t < 2:
             acti(W("g1"), W("erow"), oan)
-            acti(W("g2"), W("g1"), oan)
-        else:
-            children(0)
-            children(1)
-            fill(W("tz"), 0.0)
+
+        for b in range(3):
+            tti(W("xt", b, 4 * C, 4), col("rs", b), oan, col("fo", b), A.add)
+        for i in range(2):
+            tt(W("xt", 4 * H * i + 3, 4 * H * i + 4 * H, 4), half("vg", i), W("ps2", H * i, H * i + H), A.add)
+            quant(half("q%d" % (t + 1), i), half("qs%d" % (t + 1), i), W("xt", 4 * H * i, 4 * H * i + 4 * H))
+        if t == 2:
             tt(W("w1", 0, 24), ai, x1, A.is_equal)
             ts(W("w1", 24, 48), ai, -1.0, float(C), A.mult, A.add)
             cp(S16("tz", 1), W("cvl", 0, 24))
@@ -515,35 +532,21 @@ def rank_program(g, core, T, topo):
             tt(W("w4", 0, 24), W("w1", 0, 24), W("w1", 24, 48), A.mult)
             tt(S16("tz", 0), ai, W("w4", 0, 24), A.add)
             tr(W("trow"), W("tz"))
-            for i in range(3):
-                store("y", T.tr[:, C * i:C * i + C], W("trow"), T.trow[i:128:16, 0:C])
-            quant(W("vq"), W("vs8"), W("vt"))
-
-        for b in range(3):
-            tti(W("xt", b, 4 * C, 4), col("rs", b), oan, col("fo", b), A.add)
-        if t < 2:
-            children(0)
-        for i in range(2):
-            tt(W("xt", 4 * H * i + 3, 4 * H * i + 4 * H, 4), half("vg", i), W("ps2", H * i, H * i + H), A.add)
-            quant(half("q%d" % (t + 1), i), half("qs%d" % (t + 1), i), W("xt", 4 * H * i, 4 * H * i + 4 * H))
-        if t < 2:
-            children(1)
+        else:
             tr(W("tg", 0, C), W("g1"))
             cp(W("cvl", 48, 72), tg(0, 0))
             turn("cvl", "cal", 3, 5, "ol")
-            tr(W("tg", C, 2 * C), W("g2"))
-            cp(W("r12"), S16("tg", 0, 0, 2 * C))
-            tt(W("sa", 24, 72), S16("tg", 0, 0, 2 * C), W("r12"), A.subtract)
 
     for i in range(2):
         mm(i, H, W("vq"), W("vs8"), half("q3", i), half("qs3", i))
     store("y", T.oc[:], W("q3"), T.q3[:, 0:C].bitcast(dt.uint8))
-    act(half("yo", 0), W("ps0", 0, H))
-    cp(half("yo", 1), W("ps1", 0, H))
-    store("s", T.y[:, 0:H], half("yo", 0), T.yo[:, 0:H])
-    store("y", T.y[:, H:C], half("yo", 1), T.yo[:, H:C])
+    for i in range(2):
+        act(half("yo", i), W("ps%d" % i, 0, H))
+        store("s", T.y[:, H * i:H * i + H], half("yo", i), T.yo[:, H * i:H * i + H])
+    for i in range(3):
+        store("y", T.tr[:, C * i:C * i + C], W("trow"), T.trow[i:128:16, 0:C])
     for k in range(4):
-        store("y" if k % 2 else "s", T.osc[4 * k:4 * k + 4, 0:C], W("qs3"), T.qs3[32 * k:32 * k + 4, 0:C])
+        store("s", T.osc[4 * k:4 * k + 4, 0:C], W("qs3"), T.qs3[32 * k:32 * k + 4, 0:C])
     for t in range(3):
         count["rq%d" % t] = 2 * eight
         count["rl%d" % t] = eight

from concourse.mybir import dt, AluOpType, ActivationFunctionType

C = 384
H = C // 2
STEP = [1, 2, 4]
BIG = 2.0 ** 90
J0 = 8176.0 * 256
U = 2.0 ** -12
F32, BF, U16, I32, X4, U8 = "float32", "bfloat16", "uint16", "int32", "float8_e4m3fn_x4", "uint8"


def _sb(n, d):
    return ("sbuf", [128, n], d)


SCRATCH = {
    "xin": _sb(4 * C, BF), "ut": _sb(512, BF), "vt": _sb(512, BF), "et": _sb(2048, BF),
    "upt": _sb(24, I32), "lft": _sb(24, I32), "rtt": _sb(24, I32),
    "uq": _sb(128, X4), "us": _sb(128, U8), "vq": _sb(128, X4), "vs8": _sb(128, U8),
    "eq": _sb(512, X4), "es": _sb(512, U8), "wq": _sb(512, X4), "wsc": _sb(512, U8),
    "ml": _sb(6, U16),
    "cvi": _sb(224, F32), "cai": _sb(128, F32), "xs": _sb(80, F32),
    "cva0": _sb(224, F32), "cva1": _sb(224, F32), "caa": _sb(128, F32),
    "cvl": _sb(224, F32), "cal": _sb(128, F32),
    "wrow": _sb(400, F32), "ra": _sb(C, F32), "rl": _sb(C, F32), "rr": _sb(C, F32),
    "tbw": _sb(C, F32), "tba": _sb(C, F32), "tbl": _sb(C, F32), "tbr": _sb(C, F32),
    "td": _sb(C, F32), "drow": _sb(400, F32), "dl": _sb(C, F32), "dr": _sb(C, F32), "tb2": _sb(2 * C, F32),
    "tk": _sb(2 * C, BF), "krow": _sb(400, BF), "k4row": _sb(C, BF),
    "r3q": _sb(C, BF), "r3lr": _sb(2 * C, BF), "r3w": _sb(C, BF), "t3": _sb(4 * C, BF),
    "te": _sb(C, F32), "erow": _sb(400, F32), "el": _sb(C, F32), "er": _sb(C, F32),
    "g1": _sb(C, F32), "g2": _sb(C, F32), "g3": _sb(C, F32), "trow": _sb(C, F32),
    "tel": _sb(2 * C, F32), "tg": _sb(3 * C, F32), "tz": _sb(C, F32), "vg": _sb(C, F32),
    "fo": _sb(4 * C, BF), "zf": _sb(4 * C, BF), "zk": _sb(4 * C, BF), "zg": _sb(3 * C, BF), "zh": _sb(C, BF), "zt": _sb(4 * C, BF), "zq": _sb(C, X4), "zs": _sb(C, U8),
    "rs": _sb(4 * C, F32), "xt": _sb(4 * C, BF), "yo": _sb(C, F32),
}
_FLOATS = {"n": 72, "m1": 24, "m2": 24, "pp": 72, "pq": 72, "hh": 24, "ee": 24, "j1": 72, "jt": 72, "s3": 72, "yq": 48, "fy": 48, "yp": 48,
           "yb": 24, "ba": 24, "fv": 48, "pv": 48, "ph": 24, "cy": 48, "cvc": 48, "dy": 48, "dvc": 48, "dsy": 48, "lk": 48, "p1": 24,
           "ct": 288, "sa": 72, "w1": 48, "w2": 48, "w3": 48, "w4": 48, "w5": 48, "w6": 48, "w7": 48, "w8": 48, "w9": 48, "x2": 48, "jw": 24, "j0": 24, "mt": 32}
_WHOLES = {"kj": 48, "qi": 24, "vc": 48, "r12": 48, "alr": 48, "ai0": 24, "ai1": 24, "pi": 24, "pb": 24, "pc": 24, "p31": 24, "p15": 24,
           "pe": 24, "po": 24}
PIECE = {}
for _n, _d, _w in (("floats", F32, _FLOATS), ("wholes", I32, _WHOLES)):
    _at = 0
    for _k in _w:
        PIECE[_k] = (_n, _at, _w[_k])
        _at += _w[_k]
    SCRATCH[_n] = _sb(_at, _d)
for _t in range(4):
    SCRATCH["q%d" % _t] = _sb(C, X4)
    SCRATCH["qs%d" % _t] = _sb(C, U8)
    SCRATCH["oa%d" % _t] = _sb(32, U16)
for _t in range(3):
    SCRATCH["lq%d" % _t] = _sb(C, X4)
    SCRATCH["ls%d" % _t] = _sb(C, U8)
    SCRATCH["ll%d" % _t] = _sb(24, U16)
SCRATCH["ol"] = _sb(80, U16)
for _i in range(8):
    SCRATCH["ps%d" % _i] = ("psum", [128, 512], F32)
SEMAPHORES = ["sv", "ss", "st", "sg", "ix0", "ix1", "iu", "iv", "ip", "il", "ir", "iw", "iz", "out", "loc",
              "rq0", "rq1", "rq2", "rl0", "rl1", "rl2"]


def rank_program(g, core, T, topo):
    rank = T.rank_of(core)
    if rank is None:
        return
    A = AluOpType
    COPY = ActivationFunctionType.Copy
    N = len(T.cores)
    queues = {"v": g.vector, "s": g.scalar, "t": g.tensor, "g": g, "y": g.sync}
    own = {"v": "sv", "s": "ss", "t": "st", "g": "sg"}
    count = {k: 0 for k in SEMAPHORES}
    known = {k: {} for k in queues}
    after = {}
    seen = {}

    def join(a, b):
        for k, v in b.items():
            if a.get(k, 0) < v:
                a[k] = v

    def W(name, a=0, b=None, step=1):
        if b is None:
            b = PIECE[name][2] if name in PIECE else SCRATCH[name][1][1]
        return (name, a, b, step)

    def S16(name, k, a=0, b=C):
        return (name, a + k, b, 16)

    def ap(v):
        name, at = PIECE[v[0]][:2] if v[0] in PIECE else (v[0], 0)
        return T[name][:, at + v[1]:at + v[2]] if v[3] == 1 else T[name][:, at + v[1]:at + v[2]:v[3]]

    def over(a, b):
        if a[0][:2] == "ps":
            return True
        if a[1] >= b[2] or b[1] >= a[2]:
            return False
        return not (a[3] == b[3] and a[3] > 1 and (a[1] - b[1]) % a[3] != 0)

    def waits(qn, reads, writes):
        need = {}
        for v, w in [(v, False) for v in reads] + [(v, True) for v in writes]:
            for o, ow, oq, sem, val in seen.get(v[0], []):
                if not over(o, v):
                    continue
                if not (w or ow) and not (v[0][:2] == "ps" and oq != qn):
                    continue
                need[sem] = max(need.get(sem, 0), val)
        for sem in sorted(need, key=lambda k: -need[k]):
            if known[qn].get(sem, 0) < need[sem]:
                queues[qn].wait_ge(T.sem[sem], need[sem])
                join(known[qn], after.get((sem, need[sem]), {}))
                join(known[qn], {sem: need[sem]})

    def emit(qn, call, reads, writes):
        waits(qn, reads, writes)
        sem = own[qn]
        count[sem] += 1
        call().then_inc(T.sem[sem], 1)
        k = dict(known[qn])
        k[sem] = count[sem]
        join(k, after.get((sem, count[sem] - 1), {}))
        after[(sem, count[sem])] = k
        for v, w in [(v, False) for v in reads] + [(v, True) for v in writes]:
            seen.setdefault(v[0], []).append((v, w, qn, sem, count[sem]))

    def load(qn, dst, out, src, sem):
        count[sem] += 16
        queues[qn].dma_start(out, src).then_inc(T.sem[sem], 16)
        seen.setdefault(dst[0], []).append((dst, True, "dma", sem, count[sem]))

    def store(qn, out, src, src_ap):
        waits(qn, [src], [])
        count["out"] += 16
        queues[qn].dma_start(out, src_ap).then_inc(T.sem["out"], 16)

    def tt(out, a, b, op):
        emit("v", lambda: g.vector.tensor_tensor(ap(out), ap(a), ap(b), op), [a, b], [out])

    def tti(out, win, off, b, op):
        emit("v", lambda: g.vector.tensor_tensor(ap(out), ap(win).indirect(ap(off)), ap(b), op), [win, off, b], [out])

    def ts(out, a, s1, s2, op0, op1=None):
        if op1 is None:
            emit("v", lambda: g.vector.tensor_scalar(ap(out), ap(a), s1, None, op0), [a], [out])
        else:
            emit("v", lambda: g.vector.tensor_scalar(ap(out), ap(a), s1, s2, op0, op1), [a], [out])

    def cp(out, a):
        emit("v", lambda: g.vector.tensor_copy(ap(out), ap(a)), [a], [out])

    def cpi(out, win, off):
        emit("v", lambda: g.vector.tensor_copy(ap(out), ap(win).indirect(ap(off))), [win, off], [out])

    def tr(out, a):
        emit("v", lambda: g.vector.transpose(ap(out), ap(a)), [a], [out])

    def fill(out, c):
        emit("v", lambda: g.vector.memset(ap(out), c), [], [out])

    def quant(q, s, a):
        emit("v", lambda: g.vector.quantize_mx(ap(q), ap(s), ap(a)), [a], [q, s])

    def act(out, a, scale=1.0, bias=0.0):
        emit("s", lambda: g.scalar.activation(ap(out), ap(a), COPY, bias=bias, scale=scale), [a], [out])

    def acti(out, win, off, scale=1.0):
        emit("s", lambda: g.scalar.activation(ap(out), ap(win).indirect(ap(off)), COPY, scale=scale), [win, off], [out])

    def mm(bank, n, lq, lsc, rq, rsc):
        o = W("ps%d" % bank, 0, n)
        emit("t", lambda: g.tensor.matmul_mx(ap(o), ap(lq), ap(lsc), ap(rq), ap(rsc), True, True), [lq, lsc, rq, rsc], [o])

    def iota(out, pattern, cm):
        if out[0] in _WHOLES:
            emit("g", lambda: g.iota(ap(out), pattern, 0, cm), [], [out])
        else:
            emit("g", lambda: g.iota(ap(out), pattern, 0, cm, allow_small_or_imprecise_dtypes=True), [], [out])

    def turn(cv, ca, k, n, out):
        tr(W(ca, 16, 16 + 32 * k), W(cv, 0, 32 * k))
        spare(1)
        tr(W(cv, 96, 128 + 32 * k), W(ca, 0, 32 * k + 32))
        spare(1)
        cpi(W(out, 0, 16 * n), W(cv, 0, 128 + 32 * k), W("ml", 0, n))

    todo = []

    def spare(n):
        for _ in range(min(n, len(todo))):
            todo.pop(0)()

    def half(name, i):
        return W(name, H * i, H * i + H)

    load("y", W("xin", 0, 4 * H), T.xin[:, 0:4 * H], T.x[:, 0:4 * H], "ix0")
    load("s", W("upt"), T.upt[:], T.up[:], "ip")
    load("s", W("lft"), T.lft[:], T.lf[:], "il")
    load("s", W("rtt"), T.rtt[:], T.rt[:], "ir")
    load("y", W("xin", 4 * H, 4 * C), T.xin[:, 4 * H:4 * C], T.x[:, 4 * H:4 * C], "ix1")
    load("s", W("ut"), T.ut[:], T.u[:], "iu")
    load("y", W("wq"), T.wq[:, 0:512].bitcast(dt.uint8), T.wc[:, 0:2048], "iw")
    load("y", W("wsc"), T.wsc[:, 0:512], T.ws[:, 0:512], "iz")
    load("y", W("vt"), T.vt[:], T.v[:], "iv")

    iota(W("pi"), [[0, 24]], 1)
    iota(W("pb"), [[32, 12], [0, 2]], 0)
    iota(W("pc"), [[16, 24]], 0)
    fill(W("et", 0, 512), 1.0)
    emit("g", lambda: g.affine_select(T.et[:, 0:512], T.et[:, 0:512], [[-1, 512]], A.is_equal, 0.0, 0, 4), [W("et", 0, 512)], [W("et", 0, 512)])
    for b in ("te", "cvl", "cal", "td", "cva0"):
        iota(W(b), [[0, SCRATCH[b][1][1]]], 0)
    for b in range(1, 4):
        fill(W("et", 512 * b, 512 * b + b), 0.0)
    fill(W("cvi"), 0.0)
    fill(W("cai"), 0.0)
    ts(W("p31"), W("pi"), 31, None, A.bitwise_and)
    ts(W("p15"), W("pi"), 15, None, A.bitwise_and)
    ts(W("pe"), W("pi"), 4, 1, A.logical_shift_right, A.bitwise_and)
    ts(W("po"), W("pi"), 1, None, A.bitwise_and)
    tt(W("x2", 0, 24), W("p31"), W("pb"), A.add)
    tt(W("x2", 24, 48), W("p31"), W("pb"), A.add)
    tt(W("jw"), W("p15"), W("pc"), A.add)
    tt(W("mt", 0, 6), W("po", 0, 6), W("pe", 0, 6), A.subtract)
    ts(W("w1", 24, 48), W("jw"), float(C), None, A.subtract)
    tt(W("mt", 8, 14), W("mt", 0, 6), W("mt", 0, 6), A.mult)
    ts(W("mt", 0, 6), W("mt", 0, 6), 15.0, None, A.mult)
    ts(W("mt", 8, 14), W("mt", 8, 14), 112.0, None, A.mult)
    tt(W("mt", 16, 22), W("mt", 0, 6), W("jw", 0, 6), A.add)
    tt(W("mt", 24, 30), W("mt", 8, 14), W("mt", 16, 22), A.add)
    cp(W("ml"), W("mt", 24, 30))
    fill(W("erow", C, 400), float(C))
    for b in range(1, 4):
        act(W("et", 512 * b + b, 512 * b + 512), W("et", 0, 512 - b))

    x1 = W("x2", 0, 24)
    ts(W("w1", 0, 24), W("upt"), float(C), None, A.is_equal)
    cp(W("cvi", 24, 48), W("lft"))
    cp(W("cvi", 48, 72), W("rtt"))
    tt(W("w2", 0, 24), W("w1", 0, 24), W("w1", 24, 48), A.mult)
    tt(W("cvi", 0, 24), W("upt"), W("w2", 0, 24), A.add)
    cp(W("oa0", 0, 24), W("cvi", 0, 24))
    turn("cvi", "cai", 3, 5, "xs")
    cp(S16("te", 0), W("xs", 0, 24))
    cp(S16("te", 1), W("xs", 48, 72))
    cp(S16("te", 2), W("xs", 24, 48))
    tr(W("erow", 0, C), W("te"))
    acti(W("g1"), W("erow"), W("oa0", 0, 24))
    fill(W("wrow", C, 400), -BIG)
    cp(W("cvl", 0, 48), W("xs", 24, 72))
    quant(W("uq"), W("us"), W("ut"))

    def tg(i, k):
        return S16("tg", k, C * i, C * i + C)

    def sides(out, i, who):
        tt(W("w1", 0, 24), tg(i, 2), who, A.is_equal)
        tt(W("w1", 24, 48), tg(i, 1), who, A.is_equal)
        tt(W("w2", 0, 24), W("w1", 0, 24), W("w1", 24, 48), A.add)
        tt(W("w2", 24, 48), W("w2", 0, 24), W("w1", 24, 48), A.add)
        ts(out, W("w2", 24, 48), U, None, A.mult)

    sT, s1, s2 = [W("sa", 24 * i, 24 * i + 24) for i in range(3)]

    def ct(i):
        return W("ct", 24 * i, 24 * i + 24)

    def own_shapes():
        act(W("s3", 0, 24), sT, 256.0 / U)
        act(W("s3", 24, 48), sT, 768.0 / U, 256.0)
        act(W("s3", 48, 72), sT, 768.0 / U, 512.0)
        act(W("cy", 0, 24), sT, 768.0 / U, 4352.0)
        act(W("cy", 24, 48), sT, 768.0 / U, 8704.0)
        act(ct(0), sT, 272.0 / U)
        act(W("dsy", 0, 24), sT, -1.0 / U, 2.0)
        act(W("dsy", 24, 48), sT, -1.0 / U, 1.0)

    def upper_shapes():
        act(ct(1), s1, 48.0 / U)
        act(ct(2), s1, 17.0 / U)
        act(ct(3), s2, 3.0 / U)

    def targets(p1, p):
        return [
            lambda: tt(W("dy", 0, 24), W("lk", 0, 24), p, A.subtract),
            lambda: tt(W("dy", 24, 48), W("lk", 24, 48), p, A.subtract),
            lambda: tt(ct(4), sT, s1, A.add),
            lambda: tt(ct(6), x1, p1, A.subtract),
            lambda: ts(ct(7), s1, 0.0, None, A.is_equal),
            lambda: ts(ct(8), ct(4), 3 * U, 65536.0, A.not_equal, A.mult),
            lambda: tt(W("dvc", 24, 48), p1, p, A.subtract),
            lambda: tt(ct(9), ct(7), ct(6), A.mult),
            lambda: tt(W("cvc", 0, 24), ct(0), ct(1), A.add),
            lambda: tt(ct(10), ct(2), ct(3), A.add),
            lambda: tt(W("dvc", 0, 24), ct(9), W("dvc", 24, 48), A.add),
            lambda: tt(W("cvc", 24, 48), ct(10), ct(8), A.add)]

    for i in range(2):
        quant(half("q0", i), half("qs0", i), W("xin", 4 * H * i, 4 * H * i + 4 * H))
    tr(W("tg", 0, C), W("g1"))
    cp(W("cvl", 48, 72), tg(0, 0))
    turn("cvl", "cal", 3, 5, "ol")

    me = T.cores
    eight = min(len(topo.engines(core, d)) for d in me if d != core)

    def send(dst, out, src, sem, reads):
        waits("g", reads, [])
        rid, pid, _ = topo.addr(dst)
        e = topo.engines(core, dst)[:eight]
        g.remote_dma(out, src, T.sem[sem], T.sem["loc"], pid, rid, sum(1 << i for i in e))
        count["loc"] += len(e)

    def arrive(sem, total, names):
        for b in names:
            seen.setdefault(b, []).append((W(b), True, "far", sem, total))

    def col(n, b):
        return W(n, C * b, C * b + C)

    for t in range(3):
        q, qs, lq, ls, ll = "q%d" % t, "qs%d" % t, "lq%d" % t, "ls%d" % t, "ll%d" % t
        oa, on = W("oa%d" % t, 0, 24), "oa%d" % (t + 1)
        dst = me[(rank + STEP[t]) % N]
        send(dst, ap(W(lq)).bitcast(dt.uint8), ap(W(q)).bitcast(dt.uint8), "rq%d" % t, [W(q)])
        send(dst, ap(W(ls)), ap(W(qs)), "rq%d" % t, [W(qs)])
        arrive("rq%d" % t, 2 * eight, [lq, ls])
        arrive("rl%d" % t, eight, [ll])
        a = W("cva%d" % (t % 2), 0, 24)
        an = W("cva%d" % ((t + 1) % 2), 0, 24)
        aL, aR, aAA = W("ol", 0, 24), W("ol", 24, 48), W("ol", 48, 72)
        for i in range(2):
            mm(i, H, W("uq"), W("us"), half(q, i), half(qs, i))
            mm(6 + i, H, W("uq"), W("us"), half(q, i), half(qs, i))
        for i in range(2):
            act(half("wrow", i), W("ps%d" % i, 0, H))
        for i in range(2):
            tr(half("tbw", i), W("ps%d" % (6 + i), 0, H))
        if t == 0:
            for b in ("tk", "caa", "cva1", "tz"):
                iota(W(b), [[0, SCRATCH[b][1][1]]], 0)
            fill(W("drow", C, 400), BIG)
            fill(W("krow", C, 400), 0.0)
            ts(W("j0"), x1, -4096.0, J0, A.mult, A.add)
            cp(W("ai0"), W("xs", 0, 24))
            cp(W("jt", 0, 24), W("j0"))
            quant(W("eq"), W("es"), W("et"))
        fb = [0, 1, 6]
        for b in range(3):
            mm(fb[b], C, W("eq", 128 * b, 128 * b + 128), W("es", 128 * b, 128 * b + 128), W(q), W(qs))
        acti(W("ra"), W("wrow"), oa)
        acti(W("rl"), W("wrow"), aL)
        acti(W("rr"), W("wrow"), aR)
        if t == 0:
            sides(sT, 0, x1)
            tt(a, W("ai0"), sT, A.add)
        own_shapes()
        act(W("jt", 24, 72), W("cvl", 0, 48), -4096.0, J0)
        act(W("lk", 0, 24), W("cvl", 0, 24), 1.0, 2 * U)
        act(W("lk", 24, 48), W("cvl", 24, 48), 1.0, U)
        acti(W("g2"), W("g1"), oa)
        if t == 0:
            acti(W("g3"), W("g2"), oa)
        else:
            act(S16("te", 1), W("cvl", 24, 48))
            act(S16("te", 2), W("cvl", 0, 24))
        tr(W("tba"), W("ra"))
        w0 = S16("tbw", 0)
        tt(W("n", 0, 24), S16("tba", 0), w0, A.subtract)
        tr(W("tbl"), W("rl"))
        tt(W("n", 24, 48), w0, S16("tbl", 0), A.subtract)
        tr(W("tbr"), W("rr"))
        tt(W("m1"), W("n", 0, 24), W("n", 24, 48), A.min)
        tt(W("n", 48, 72), w0, S16("tbr", 0), A.subtract)
        act(col("fo", 0), W("ps%d" % fb[0], 0, C))
        M = S16("td", 0)
        tt(M, W("m1"), W("n", 48, 72), A.min)
        tt(W("j1"), W("jt"), W("s3"), A.add)
        for i in range(3):
            tt(W("pp", 24 * i, 24 * i + 24), W("n", 24 * i, 24 * i + 24), M, A.is_le)
        tt(W("pq"), W("pp"), W("j1"), A.mult)
        tt(W("hh"), W("pq", 0, 24), W("pq", 24, 48), A.max)
        tt(S16("td", 1), W("hh"), W("pq", 48, 72), A.max)
        tr(W("drow", 0, C), W("td"))
        acti(W("dl"), W("drow"), aL)
        acti(W("dr"), W("drow"), aR)
        for b in range(1, 3):
            act(col("fo", b), W("ps%d" % fb[b], 0, C))
        tr(W("tg", C, 2 * C), W("g2"))
        if t == 0:
            tr(W("tg", 2 * C, 3 * C), W("g3"))
            sides(s1, 1, W("ai0"))
            sides(s2, 2, W("cvl", 48, 72))
            tt(W("p1"), W("cvl", 48, 72), s1, A.add)
        else:
            cp(W("r12"), S16("tg", 0, 0, 2 * C))
            tt(W("sa", 24, 72), S16("tg", 0, 0, 2 * C), W("r12"), A.subtract)
        upper_shapes()
        todo.extend(targets(W("p1") if t == 0 else tg(0, 0), a))
        spare(1)
        tr(W("tb2", 0, C), W("dl"))
        nl, nr = S16("tb2", 0), S16("tb2", 0, C, 2 * C)
        tt(W("m1"), W("n", 0, 24), nl, A.min)
        tr(W("tb2", C, 2 * C), W("dr"))
        spare(1)
        tt(W("m2"), W("m1"), nr, A.min)
        spare(1)
        tt(W("pp", 24, 48), nl, W("m2"), A.is_le)
        tt(W("pp", 48, 72), nr, W("m2"), A.is_le)
        tt(W("pp", 0, 24), W("n", 0, 24), W("m2"), A.is_le)
        tt(W("pq", 24, 72), W("pp", 24, 72), S16("tb2", 1, 0, 2 * C), A.mult)
        tt(W("pq", 0, 24), W("pp", 0, 24), W("j0"), A.mult)
        tt(W("hh"), W("pq", 24, 48), W("pq", 48, 72), A.max)
        ts(W("ee"), W("m2"), 0.0, 3840.0, A.is_ge, A.mult)
        tt(W("kj", 0, 24), W("hh"), W("pq", 0, 24), A.max)
        spare(1)
        ts(W("kj", 24, 48), W("kj", 0, 24), 0xF00, None, A.bitwise_and)
        spare(1)
        tt(S16("tk", 0), W("kj", 24, 48), W("ee"), A.max)
        spare(1)
        tr(W("krow", 0, C), W("tk", 0, C))
        ts(S16("tk", 0, C, 2 * C), S16("tk", 0), 16.0, None, A.mult)
        spare(1)
        tr(W("k4row"), W("tk", C, 2 * C))
        spare(1)
        acti(W("r3lr"), W("krow"), W("ol", 0, 48), 1.0 / 256)
        tti(W("r3q"), W("krow"), oa, W("k4row"), A.add)
        acti(W("r3w"), W("r3q"), aAA, 1.0 / 256)
        spare(1)
        tr(W("t3", 0, C), W("r3q"))
        spare(1)
        q2 = S16("t3", 0, 0, C)
        tr(W("t3", C, 3 * C), W("r3lr"))
        spare(1)
        tt(W("yq", 0, 24), S16("t3", 0, C, 2 * C), q2, A.add)
        tt(W("yq", 24, 48), S16("t3", 0, 2 * C, 3 * C), q2, A.add)
        spare(1)
        tt(W("fy"), W("yq"), W("cy"), A.is_equal)
        spare(1)
        tt(W("yp"), W("fy"), W("dy"), A.mult)
        tr(W("t3", 3 * C, 4 * C), W("r3w"))
        tt(W("hh"), W("yp", 0, 24), W("yp", 24, 48), A.add)
        tt(W("qi"), S16("t3", 0, 3 * C, 4 * C), q2, A.add)
        tt(W("ba"), W("hh"), a, A.add)
        ts(W("vc", 0, 24), W("qi"), 0xFFF0, None, A.bitwise_and)
        ts(W("vc", 24, 48), W("qi"), 0x0FFF, None, A.bitwise_and)
        spare(len(todo))
        tt(W("fv"), W("vc"), W("cvc"), A.is_equal)
        tt(W("yb"), W("fy", 0, 24), W("fy", 24, 48), A.add)
        tt(W("pv"), W("fv"), W("dvc"), A.mult)
        tt(W("w1", 0, 24), W("yb"), W("fv", 24, 48), A.add)
        tt(W("ph"), W("pv", 0, 24), W("pv", 24, 48), A.add)
        tt(an, W("ph"), W("ba"), A.add)
        ao, ai = W("ai%d" % (t % 2)), W("ai%d" % ((t + 1) % 2))
        todo.extend([lambda: cp(ai, an), lambda: cp(S16("te", 0), an)])
        turn(an[0], "caa", 1, 2, on)
        send(dst, ap(W(ll)), ap(W(on, 0, 24)), "rl%d" % t, [W(on)])
        oan = W(on, 0, 24)

        for b in range(4):
            mm(2 + b, C, W("eq", 128 * b, 128 * b + 128), W("es", 128 * b, 128 * b + 128), W(lq), W(ls))
        for b in range(4):
            act(col("zf", b), W("ps%d" % (2 + b), 0, C), 0.5)

        tt(W("w1", 24, 48), ai, x1, A.subtract)
        tt(W("w2", 0, 24), W("w1", 0, 24), W("w1", 24, 48), A.mult)
        tt(S16("te", 3), W("w2", 0, 24), x1, A.add)
        tr(W("erow", 0, C), W("te"))
        acti(W("el"), W("erow"), aL)
        acti(W("er"), W("erow"), aR)
        if t < 2:
            tt(sT, an, ai, A.subtract)
        else:
            quant(W("vq"), W("vs8"), W("vt"))
        tt(W("w3", 0, 24), W("fv", 0, 24), W("dsy", 24, 48), A.mult)
        tt(W("w3", 24, 48), W("fv", 0, 24), W("dsy", 0, 24), A.mult)
        for b in range(3):
            cp(col("zg", b), col("zf", b))
        tr(W("tel", 0, C), W("el"))
        tr(W("tel", C, 2 * C), W("er"))

        off = W(ll)
        acti(col("zk", 3), col("zf", 3), off)
        for b in range(3):
            tti(col("zk", b), col("zf", b), off, col("zg", b), A.add)
            if b == 0:
                emit("g", lambda: g.affine_select(T.zh[:], T.zk[:, 3 * C:4 * C], [[1, C]], A.is_ge, 0.0, 0, 1), [col("zk", 3)], [W("zh")])
            if b < 2:
                acti(W("zt", b, 4 * C, 4), col("zk", b), off)
        for i in range(2):
            oh = W(ll, 12 * i, 12 * i + 12)
            acti(W("zt", 4 * H * i + 2, 4 * H * i + 4 * H, 4), col("zk", 2), oh)
            tti(W("zt", 4 * H * i + 3, 4 * H * i + 4 * H, 4), col("zk", 3), oh, half("zh", i), A.add)
        rb = [[2, 3, 4, 5], [6, 7, 0, 1]]
        for i in range(2):
            quant(half("zq", i), half("zs", i), W("zt", 4 * H * i, 4 * H * i + 4 * H))

        for b in range(4):
            for i in range(2):
                mm(rb[i][b], H, W("wq", 128 * b, 128 * b + 128), W("wsc", 128 * b, 128 * b + 128), half("zq", i), half("zs", i))
        for b in range(4):
            for i in range(2):
                act(W("rs", C * b + H * i, C * b + H * i + H), W("ps%d" % rb[i][b], 0, H), 0.03125)

        lr = W("cvl", 0, 48)
        lz, lzl, lzr = S16("tel", 3, 0, 2 * C), S16("tel", 3), S16("tel", 3, C, 2 * C)
        tt(W("w1", 0, 24), S16("tel", 1), lzl, A.subtract)
        tt(W("w1", 24, 48), S16("tel", 2, C, 2 * C), lzr, A.subtract)
        tt(W("w2", 0, 24), lzl, ao, A.subtract)
        tt(W("w2", 24, 48), ao, lzr, A.subtract)
        tt(W("w4"), W("fy"), W("w1"), A.mult)
        tt(W("w6"), W("w3"), W("w2"), A.mult)
        tt(W("w7"), lz, W("w4"), A.add)
        tt(lr, W("w7"), W("w6"), A.add)
        for i in range(2):
            acti(half("vg", i), col("rs", 3), W(on, 12 * i, 12 * i + 12))
        mm(2, C, W("eq", 384, 512), W("es", 384, 512), W(q), W(qs))
        if t < 2:
            acti(W("g1"), W("erow"), oan)

        for b in range(3):
            tti(W("xt", b, 4 * C, 4), col("rs", b), oan, col("fo", b), A.add)
        for i in range(2):
            tt(W("xt", 4 * H * i + 3, 4 * H * i + 4 * H, 4), half("vg", i), W("ps2", H * i, H * i + H), A.add)
            quant(half("q%d" % (t + 1), i), half("qs%d" % (t + 1), i), W("xt", 4 * H * i, 4 * H * i + 4 * H))
        if t == 2:
            tt(W("w1", 0, 24), ai, x1, A.is_equal)
            ts(W("w1", 24, 48), ai, -1.0, float(C), A.mult, A.add)
            cp(S16("tz", 1), W("cvl", 0, 24))
            cp(S16("tz", 2), W("cvl", 24, 48))
            tt(W("w4", 0, 24), W("w1", 0, 24), W("w1", 24, 48), A.mult)
            tt(S16("tz", 0), ai, W("w4", 0, 24), A.add)
            tr(W("trow"), W("tz"))
        else:
            tr(W("tg", 0, C), W("g1"))
            cp(W("cvl", 48, 72), tg(0, 0))
            turn("cvl", "cal", 3, 5, "ol")

    for i in range(2):
        mm(i, H, W("vq"), W("vs8"), half("q3", i), half("qs3", i))
    store("y", T.oc[:], W("q3"), T.q3[:, 0:C].bitcast(dt.uint8))
    for i in range(2):
        act(half("yo", i), W("ps%d" % i, 0, H))
        store("s", T.y[:, H * i:H * i + H], half("yo", i), T.yo[:, H * i:H * i + H])
    for i in range(3):
        store("y", T.tr[:, C * i:C * i + C], W("trow"), T.trow[i:128:16, 0:C])
    for k in range(4):
        store("s", T.osc[4 * k:4 * k + 4, 0:C], W("qs3"), T.qs3[32 * k:32 * k + 4, 0:C])
    for t in range(3):
        count["rq%d" % t] = 2 * eight
        count["rl%d" % t] = eight
    for sem in SEMAPHORES:
        if known["g"].get(sem, 0) < count[sem]:
            g.wait_ge(T.sem[sem], count[sem])
